import numpy as np, ml_dtypes
CORES = [66,74,82,90,194,202,210,218]
N = 8
BF = ml_dtypes.bfloat16
def f(rng, *shape):
    return (rng.standard_normal(shape, dtype=np.float32) * np.exp2(rng.integers(-2, 3, shape[:-1] + (1,)))).astype(BF)
def wide(rng, *shape):
    v = f(rng, *shape).astype(np.float32); k = shape[:-2] + (1, shape[-1])
    return (v * np.exp2(rng.integers(-6, 7, k)) * (rng.random(k) > 0.0625)).astype(BF)
def gentries(a):
    return np.ascontiguousarray(a.reshape(8, 16, -1).transpose(0, 2, 1)).reshape(8, -1)
def gtable(e):
    e = np.asarray(e); return np.ascontiguousarray(e.reshape(8, -1, 16).transpose(0, 2, 1)).reshape(128, -1).astype(np.int32)
WAY = "abc"; W = len(WAY)
IC, CG, CAPP, TOT, S = 2048, 256, 256, 2048, 256
def numbers(a):
    return np.stack([gentries(u) for u in a])
def slots(a):
    return np.stack([gentries(u) for u in a]).reshape(N, N, CAPP)
def columns(t, a):
    e = slots(a); t = t.astype(np.float64)
    return np.stack([np.concatenate([t[q][:, e[q, r]] for q in range(N)], axis=1) for r in range(N)])
def sums(t, x):
    return np.stack([np.bincount(x, weights=t[o], minlength=TOT) for o in range(16)])
def home(p, a):
    e = slots(a); y = np.zeros((N, 16, IC), np.float64)
    for q in range(N):
        for r in range(N):
            y[q][:, e[q, r]] += p[r][:, q * CAPP:(q + 1) * CAPP]
    return y
def anyslots(rng):
    return np.argsort(rng.random((W, N, N, IC)), axis=-1)[..., :CAPP]
def anynumbers(rng):
    x = rng.integers(0, TOT, (W, N, 8, S)); few = rng.integers(0, TOT, (W, N, 8, 32))
    return np.where(rng.random(x.shape) < 0.5, np.take_along_axis(few, rng.integers(0, 32, x.shape), axis=-1), x)
def make(rng, x, e):
    o = np.argsort(x[0], axis=-1, kind="stable"); x = np.stack([np.take_along_axis(u, o, axis=-1) for u in x])
    ob = np.lexsort((rng.random(x[1].shape), x[1]), axis=-1)
    d = {"f" + c: f(rng, N, 16, IC) for c in WAY}
    d["v"] = (rng.standard_normal((N, 8, S)) * np.exp2(rng.integers(-1, 2, (N, 8, 1)))).astype(np.float32)
    for w, c in enumerate(WAY): d["x" + c] = np.stack([gtable(u) for u in x[w]])
    d["ob"] = np.stack([gtable(u) for u in ob])
    for w, c in enumerate(WAY): d["l" + c] = np.stack([gtable(u.reshape(8, CG)) for u in e[w]])
    return d
def setup_inputs(rng):
    return make(rng, anynumbers(rng), anyslots(rng))
def setup_inputs_runs(rng):
    x = anynumbers(rng); h = rng.integers(0, TOT, (W, N, 8, 1))
    for w in range(W): x[w, :, :, w * S // 8:w * S // 8 + S // 2] = h[w]
    x[0, :, 0:2] = h[0, :, 0:1]; x[1, :, 1:3] = h[1, :, 1:2]
    return make(rng, x, anyslots(rng))
def setup_inputs_apart(rng):
    x = np.argsort(rng.random((W, N, 8 * S // TOT, TOT)), axis=-1).reshape(W, N, 8, S)
    return make(rng, x, anyslots(rng))
def setup_inputs_ends(rng):
    x = rng.integers(0, N, (W, N, 8, S)) * CAPP + rng.integers(0, 2, (W, N, 8, S)) * (CAPP - 1)
    x = np.where(rng.random(x.shape) < 0.75, x, rng.integers(0, TOT, x.shape)); x[..., 0] = 0; x[..., 1] = TOT - 1
    e = 1 + np.argsort(rng.random((W, N, N, IC - 2)), axis=-1)[..., :CAPP]; e[..., 0] = IC - 1; e[..., -1] = 0
    return make(rng, x, e)
def setup_inputs_alike(rng):
    x = anynumbers(rng); x[:, :, 1:] = x[:, :, :1].copy()
    e = np.repeat(np.argsort(rng.random((W, N, 1, IC)), axis=-1)[..., :CAPP], N, axis=2)
    return make(rng, x, e)
def setup_inputs_spread(rng):
    d = setup_inputs(rng)
    for c in WAY[1:]: d["f" + c] = wide(rng, N, 16, IC)
    return d
def check_inputs(d):
    bad = []
    for c in WAY:
        x = numbers(d["x" + c]); e = slots(d["l" + c])
        if not np.isfinite(d["f" + c].astype(np.float32)).all(): bad.append("finite_f" + c)
        if x.min() < 0 or x.max() >= TOT: bad.append("range_x" + c)
        if e.min() < 0 or e.max() >= IC: bad.append("range_l" + c)
        if (np.diff(np.sort(e, axis=-1), axis=-1) == 0).any(): bad.append("different_l" + c)
    if not np.isfinite(d["v"]).all(): bad.append("finite_v")
    if (np.diff(numbers(d["xa"]), axis=-1) < 0).any(): bad.append("sorted_xa")
    o = numbers(d["ob"])
    if not (np.sort(o, axis=-1) == np.arange(S)).all(): bad.append("places_ob")
    elif (np.diff(np.take_along_axis(numbers(d["xb"]), o, axis=-1), axis=-1) < 0).any(): bad.append("sorted_xb_by_ob")
    return bad
def reference(fa, fb, fc, v, xa, xb, xc, ob, la, lb, lc):
    xi = numbers(xa).reshape(N, 8 * S); xj = numbers(xb).reshape(N, 8 * S)
    w = np.repeat(v.astype(np.float64).reshape(N, 1, 8 * S), 16, axis=1)
    for t, x, a in ((fc, xc, lc),):
        u = columns(t, a); x = numbers(x).reshape(N, 8 * S)
        w = w * np.stack([u[r][:, x[r]] for r in range(N)])
    u = columns(fb, lb)
    ya = fa.astype(np.float64) * home([sums(w[r] * u[r][:, xj[r]], xi[r]) for r in range(N)], la)
    u = columns(ya, la)
    yb = home([sums(w[r] * u[r][:, xi[r]], xj[r]) for r in range(N)], lb)
    return {"ya": ya.astype(np.float32), "yb": yb.astype(np.float32)}

@@ -1,0 +1,439 @@
+import numpy as np
+from concourse.bass import DstId, RemoteDMATransfer
+from concourse.mybir import AluOpType, ActivationFunctionType
+
+F32, BF, I32, U16 = "float32", "bfloat16", "int32", "uint16"
+SCRATCH = {
+    "pi": ("sbuf", [128, 8], I32), "pm": ("sbuf", [128, 8], I32), "pf": ("sbuf", [128, 8], F32),
+    "pq": ("sbuf", [128, 8], F32), "ofc": ("sbuf", [128, 8], F32), "ofu": ("sbuf", [128, 8], U16),
+    "jm": ("sbuf", [128, 128], F32), "k8": ("sbuf", [128, 8], F32), "m8": ("sbuf", [128, 8], F32),
+    "em": ("sbuf", [8, 128], F32), "e8": ("sbuf", [8, 128], F32),
+    "iot": ("sbuf", [128, 2048], F32), "a16": ("sbuf", [128, 256], F32),
+    "selb": ("sbuf", [128, 1024], BF), "ident": ("sbuf", [128, 128], F32),
+    "q15": ("sbuf", [128, 128], F32), "n15": ("sbuf", [128, 128], F32),
+    "sh1": ("sbuf", [128, 128], F32), "sh15": ("sbuf", [128, 128], F32),
+    "trb": ("sbuf", [128, 16], F32), "tr": ("sbuf", [128, 16], F32),
+    "li": ("sbuf", [128, 48], I32), "xi": ("sbuf", [128, 64], I32), "v8": ("sbuf", [8, 256], F32),
+    "fbc": ("sbuf", [128, 2048], BF), "far": ("sbuf", [128, 2048], BF), "fa2": ("sbuf", [128, 256], BF),
+    "lhb": ("sbuf", [128, 48], BF), "llb": ("sbuf", [128, 48], BF),
+    "rep": ("sbuf", [128, 256], F32), "lau": ("sbuf", [128, 128], U16),
+    "lt": ("sbuf", [128, 32], U16), "lu": ("sbuf", [128, 48], U16), "xu": ("sbuf", [128, 64], U16),
+    "xk": ("sbuf", [128, 32], I32), "xq": ("sbuf", [128, 32], I32),
+    "e1": ("sbuf", [128, 32], F32), "e2": ("sbuf", [128, 32], F32), "obc": ("sbuf", [128, 32], U16),
+    "ahb": ("sbuf", [128, 16], BF), "alb": ("sbuf", [128, 16], BF),
+    "cu": ("sbuf", [128, 128], F32), "l3": ("sbuf", [128, 128], U16),
+    "xaf": ("sbuf", [128, 256], F32), "xbf": ("sbuf", [128, 256], F32),
+    "xa2": ("sbuf", [128, 256], F32), "xb2": ("sbuf", [128, 256], F32),
+    "same1": ("sbuf", [128, 256], F32), "same2": ("sbuf", [128, 256], F32),
+    "xf1": ("sbuf", [128, 24], F32), "xf2": ("sbuf", [128, 24], F32), "xd": ("sbuf", [128, 16], F32),
+    "of1": ("sbuf", [128, 16], U16), "of2": ("sbuf", [128, 16], U16),
+    "nq": ("sbuf", [128, 16], F32), "td": ("sbuf", [128, 16], F32),
+    "da0": ("sbuf", [128, 256], F32), "da1": ("sbuf", [128, 128], F32), "da2": ("sbuf", [128, 64], F32),
+    "da3": ("sbuf", [128, 32], F32),
+    "db0": ("sbuf", [128, 256], F32), "db1": ("sbuf", [128, 128], F32), "db2": ("sbuf", [128, 64], F32),
+    "db3": ("sbuf", [128, 32], F32),
+    "vf": ("sbuf", [128, 256], F32), "sb1": ("sbuf", [128, 512], BF), "land1": ("sbuf", [128, 512], BF),
+    "wb": ("sbuf", [128, 2048], BF), "wc": ("sbuf", [128, 2048], BF),
+    "w": ("sbuf", [128, 256], F32), "w2": ("sbuf", [128, 256], F32), "w2t": ("sbuf", [128, 256], F32),
+    "p1": ("sbuf", [128, 256], F32), "c1": ("sbuf", [128, 256], F32),
+    "win1": ("sbuf", [128, 2304], F32), "win2": ("sbuf", [128, 2048], F32),
+    "win3": ("sbuf", [128, 2304], F32), "win4": ("sbuf", [128, 2048], F32),
+    "sb2": ("sbuf", [128, 256], F32), "land2": ("sbuf", [128, 256], F32), "r2": ("sbuf", [128, 256], F32),
+    "fag": ("sbuf", [128, 256], F32), "fat": ("sbuf", [128, 256], F32), "gb2": ("sbuf", [128, 2048], F32),
+    "sb3": ("sbuf", [128, 256], F32), "land3": ("sbuf", [128, 256], F32), "r3": ("sbuf", [128, 272], F32),
+    "gb3": ("sbuf", [128, 2048], F32), "pt": ("sbuf", [128, 256], F32), "c2": ("sbuf", [128, 256], F32),
+    "sb4": ("sbuf", [128, 256], F32), "land4": ("sbuf", [128, 256], F32), "r4": ("sbuf", [128, 256], F32),
+    "ta": ("sbuf", [128, 256], F32), "ya0": ("sbuf", [128, 128], F32), "ya1": ("sbuf", [128, 128], F32),
+    "tb": ("sbuf", [128, 256], F32), "yb0": ("sbuf", [128, 128], F32), "yb1": ("sbuf", [128, 128], F32),
+}
+for _b in range(8):
+    SCRATCH["ps%d" % _b] = ("psum", [128, 512], F32)
+SEMAPHORES = ["qg", "qv", "qs", "qt", "dl", "db", "dc", "dx", "dv", "da", "df", "do",
+              "arr1", "arr2", "arr3", "arr4", "sent"]
+
+
+def rank_program(g, core, T, topo):
+    me = T.rank_of(core)
+    if me is None:
+        return
+    cores = T.cores
+    n_ranks = len(cores)
+    Op = AluOpType
+    COPY, IDENT = ActivationFunctionType.Copy, ActivationFunctionType.Identity
+    Q = {"g": g, "v": g.vector, "s": g.scalar, "t": g.tensor, "y": g.sync}
+    count, known, snap, written, readers = {}, {q: {} for q in Q}, {}, {}, {}
+    turn = [(me + 1 + i) % n_ranks for i in range(n_ranks)]
+
+    def learn(q, tok):
+        name, n = tok
+        if known[q].get(name, 0) < n:
+            known[q][name] = n
+        for k, m in snap.get(tok, {}).items():
+            if known[q].get(k, 0) < m:
+                known[q][k] = m
+
+    def need(q, toks):
+        for tok in sorted(set(toks), key=lambda t: (-t[1], t[0])):
+            if known[q].get(tok[0], 0) < tok[1]:
+                Q[q].wait_ge(T.sem[tok[0]], tok[1])
+                learn(q, tok)
+
+    def before(q, reads, writes):
+        toks = [written[k] for k in reads if k in written]
+        for k in writes:
+            if k in written and not (q == "t" and written[k][0] == "qt"):
+                toks.append(written[k])
+            toks += [t for t in readers.get(k, []) if t[0] != "q" + q]
+        need(q, toks)
+
+    def after(tok, reads, writes):
+        for k in reads:
+            readers.setdefault(k, []).append(tok)
+        for k in writes:
+            written[k] = tok
+            readers[k] = []
+
+    def op(q, reads, writes, fn):
+        before(q, reads, writes)
+        name = "q" + q
+        count[name] = count.get(name, 0) + 1
+        fn(Q[q]).then_inc(T.sem[name], 1)
+        tok = (name, count[name])
+        snap[tok] = dict(known[q])
+        after(tok, reads, writes)
+
+    def dma(q, sem, reads, key, out, in_):
+        before(q, reads, [])
+        Q[q].dma_start(out, in_).then_inc(T.sem[sem], 16)
+        count[sem] = count.get(sem, 0) + 16
+        if key:
+            written[key] = (sem, count[sem])
+
+    def tt(reads, writes, out, a, b, o):
+        op("v", reads, writes, lambda e: e.tensor_tensor(out, a, b, o))
+
+    def ts(reads, writes, out, a, s1, s2, o0, o1=None):
+        if o1 is None:
+            op("v", reads, writes, lambda e: e.tensor_scalar(out, a, s1, None, o0))
+        else:
+            op("v", reads, writes, lambda e: e.tensor_scalar(out, a, s1, s2, o0, o1))
+
+    def copy(q, reads, writes, out, in_):
+        if q == "v":
+            op("v", reads, writes, lambda e: e.tensor_copy(out, in_))
+        else:
+            op("s", reads, writes, lambda e: e.activation(out, in_, COPY))
+
+    def fill(key, out, c):
+        op("v", [], [key], lambda e: e.memset(out, c))
+
+    def mm(reads, writes, out, lhs, rhs, start=True, stop=True):
+        op("t", reads, writes, lambda e: e.matmul(out, lhs, rhs, start, stop))
+
+    def transpose(reads, writes, out, in_):
+        op("t", reads + ["ident"], writes, lambda e: e.transpose(out, in_, T.ident[:, :]))
+
+    def zero(win):
+        op("s", IOT, [win], lambda e: e.activation(T[win][:, 0:2048], T.iot[:, 0:2048], COPY, scale=0.0))
+
+    def send(x, half, width, reads, src, land):
+        before("g", reads, [])
+        trs = []
+        for i in ((0, 1, 2, 3), (4, 5, 6))[half]:
+            d = cores[turn[i]]
+            rid, pid = topo.addr(d, core)
+            eng = topo.engines(core, d)[2 * (i % 4):2 * (i % 4) + 2]
+            trs.append(RemoteDMATransfer(
+                dst_ids=[DstId(rid=rid, pnc=pid)], dma_engine_mask=sum(1 << e for e in eng), remote_sem=T.sem["arr%d" % x],
+                srcs=[src[:, i * width:(i + 1) * width]], dsts=[land[:, me * width:(me + 1) * width]], alu_op=0))
+        g.remote_dma_fused(trs, local_sem=T.sem.sent)
+        count["sent"] = count.get("sent", 0) + 2 * len(trs)
+        if half:
+            count["arr%d" % x] = 2 * (n_ranks - 1)
+            written["in%d" % x] = ("arr%d" % x, 2 * (n_ranks - 1))
+            copy("v", reads, ["own%d" % x], land[:, me * width:(me + 1) * width], src[:, 7 * width:8 * width])
+
+    PS = [T["ps%d" % b] for b in range(8)]
+
+    dma("y", "dl", [], "li", T.li[:, 0:16], T.lb[:, :])
+    dma("s", "dl", [], "li", T.li[:, 16:32], T.lc[:, :])
+    dma("y", "dl", [], "li", T.li[:, 32:48], T.la[:, :])
+    for k in range(4):
+        dma("y", "db", [], "fb", T.fbc[16 * k:16 * k + 16, :], T.fb[:, :])
+        dma("s", "dc", [], "fc", T.fbc[64 + 16 * k:80 + 16 * k, :], T.fc[:, :])
+    dma("y", "dx", [], "xi", T.xi[:, 0:16], T.xa[:, :])
+    dma("s", "dx", [], "xi", T.xi[:, 16:32], T.xb[:, :])
+    dma("y", "dx", [], "xi", T.xi[:, 32:48], T.xc[:, :])
+    dma("y", "dx", [], "xi", T.xi[:, 48:64], T.ob[:, :])
+    dma("y", "dv", [], "v8", T.v8[:, :], T.v[:, :])
+    for k in range(8):
+        dma("y", "da", [], "fa", T.far[16 * k:16 * k + 16, :], T.fa[:, :])
+    for h in range(2):
+        dma("y", "df", [], "fa2", T.fa2[:, 128 * h:128 * h + 128], T.fa[8 * h:8 * h + 8, :])
+
+    fl = {"allow_small_or_imprecise_dtypes": True}
+    op("g", [], ["pi"], lambda e: e.iota(T.pi[:, 0:1], [[0, 1]], 0, 1))
+    op("g", [], ["k8"], lambda e: e.iota(T.k8[:, :], [[1, 8]], 0, 0, **fl))
+    op("g", [], ["jm"], lambda e: e.iota(T.jm[:, :], [[0, 8], [1, 16]], 0, 0, **fl))
+    op("g", [], ["iot0"], lambda e: e.iota(T.iot[:, 0:256], [[1, 256]], 0, 0, **fl))
+    op("g", [], ["iot1024"], lambda e: e.iota(T.iot[:, 1024:2048], [[1, 1024]], 1024, 0, **fl))
+    pf = T.pf[:, 0:1]
+
+    def bits(j, m):
+        ts(["pi"], ["pm%d" % j], T.pm[:, j:j + 1], T.pi[:, 0:1], m, None, Op.bitwise_and)
+
+    bits(4, 15)
+    ts(["pi"], ["pm5"], T.pm[:, 5:6], T.pi[:, 0:1], 4, None, Op.logical_shift_right)
+    copy("v", ["pi"], ["pf"], pf, T.pi[:, 0:1])
+    copy("v", ["pm4", "pm5"], ["pq45"], T.pq[:, 4:6], T.pm[:, 4:6])
+    bits(0, 12)
+    bits(2, 240)
+    ts(["k8", "pq45"], ["m8"], T.m8[:, :], T.k8[:, :], T.pq[:, 5:6], None, Op.is_equal)
+    ts(["jm", "pq45"], ["a16"], T.a16[:, 0:128], T.jm[:, :], T.pq[:, 4:5], None, Op.is_equal)
+    ts(["pm2", "pf"], ["pq0"], T.pq[:, 0:1], T.pm[:, 2:3], -0.75, pf, Op.mult, Op.add)
+    for k in range(8):
+        if k % 2:
+            op("s", ["a16", "m8"], ["sel%d" % k], lambda e, k=k: e.activation(
+                T.selb[:, 128 * k:128 * k + 128], T.a16[:, 0:128], COPY, scale=T.m8[:, k:k + 1]))
+        else:
+            ts(["a16", "m8"], ["sel%d" % k], T.selb[:, 128 * k:128 * k + 128], T.a16[:, 0:128], T.m8[:, k:k + 1],
+               None, Op.mult)
+        if k == 2:
+            ts(["pm0", "pq0"], ["ofc"], T.ofc[:, 0:1], T.pm[:, 0:1], 7.0, T.pq[:, 0:1], Op.mult, Op.add)
+        if k == 6:
+            copy("v", ["ofc"], ["ofu"], T.ofu[:, 0:1], T.ofc[:, 0:1])
+    SEL = ["sel%d" % k for k in range(8)]
+    for a, b in ((256, 512), (512, 1024)):
+        op("s", ["iot0", "iot%d" % (a // 2)], ["iot%d" % a],
+           lambda e, a=a, b=b: e.activation(T.iot[:, a:b], T.iot[:, 0:b - a], IDENT, bias=float(a)))
+    IOT = ["iot0", "iot256", "iot512", "iot1024"]
+
+    def to_groups(reads, bank, col, n, r, hi, lo):
+        out = PS[bank][:, col:col + n]
+        mm(reads + [SEL[r]], ["P%d" % bank], out, T.selb[:, 128 * r:128 * r + 128], hi, True, False)
+        mm(reads + [SEL[r]], ["P%d" % bank], out, T.selb[:, 128 * r:128 * r + 128], lo, False, True)
+
+    copy("v", ["li"], ["lhb"], T.lhb[:, :], T.li[:, :])
+    tt(["li", "lhb"], ["llb"], T.llb[:, :], T.li[:, :], T.lhb[:, :], Op.subtract)
+    for i, r in enumerate(turn):
+        to_groups(["lhb", "llb"], 2 * (i // 4), 32 * (i % 4), 32, r, T.lhb[:, 0:32], T.llb[:, 0:32])
+
+    def deal(h):
+        copy("v", ["rep%d" % h, "ofu"], ["lt%d" % h], T["lt"][:, 16 * h:16 * h + 16],
+             T.rep[:, 128 * h:128 * h + 128].indirect(T.ofu[:, 0:1]))
+
+    def columns(h):
+        for q, a in (("v", 16 * h), ("s", 16 * h + 8)):
+            copy(q, ["fb", "fc", "lt%d" % h], ["sb1%s%d" % (q, h)], T.sb1[:, 16 * a:16 * a + 128],
+                 T.fbc[:, :].indirect(T["lt"][:, a:a + 8]))
+
+    copy("v", ["P0"], ["rep0"], T.rep[:, 0:128], PS[0][:, 0:128])
+    deal(0)
+    copy("v", ["P2"], ["rep1"], T.rep[:, 128:256], PS[2][:, 0:128])
+    columns(0)
+    send(1, 0, 64, ["sb1v0", "sb1s0"], T.sb1, T.land1)
+    deal(1)
+    columns(1)
+    send(1, 1, 64, ["sb1v1", "sb1s1"], T.sb1, T.land1)
+
+    op("g", [], ["em"], lambda e: e.iota(T.em[:, :], [[1, 8], [0, 16]], 0, 0, **fl))
+    op("g", [], ["trb"], lambda e: e.iota(T.trb[:, :], [[16, 16]], 2048, 0, **fl))
+    zero("win1")
+
+    def shifted(xf, keys, bank):
+        mm(keys + ["sh1"], ["P%d" % bank], PS[bank][:, 0:16], T.sh1[:, :], xf[:, 0:16], True, False)
+        mm(keys + ["sh15"], ["P%d" % bank], PS[bank][:, 0:16], T.sh15[:, :], xf[:, 1:17], False, True)
+
+    def ends(xf, keys, of, bank, between):
+        a, b, c = between
+        tt(keys + ["tr"], ["td"], T.td[:, :], xf[:, 0:16], T.tr[:, :], Op.subtract)
+        tt(["P%d" % bank] + keys, ["nq"], T.nq[:, :], PS[bank][:, 0:16], xf[:, 0:16], Op.not_equal)
+        a()
+        tt(["td", "nq"], ["td"], T.td[:, :], T.td[:, :], T.nq[:, :], Op.mult)
+        b()
+        tt(["td", "tr"], ["td"], T.td[:, :], T.td[:, :], T.tr[:, :], Op.add)
+        c()
+        copy("v", ["td"], [of], T[of][:, :], T.td[:, :])
+
+    ts(["xi"], ["xk"], T.xk[:, :], T.xi[:, 16:48], 192, None, Op.bitwise_and)
+    ts(["xi"], ["xq"], T.xq[:, :], T.xi[:, 16:48], 1792, None, Op.bitwise_and)
+    copy("v", ["xi"], ["xu"], T.xu[:, :], T.xi[:, :])
+    copy("v", ["xi"], ["xf1"], T.xf1[:, 0:16], T.xi[:, 0:16])
+    fill("xf1e", T.xf1[:, 16:24], -1.0)
+    ts(["jm"], ["n15"], T.n15[:, :], T.jm[:, :], 15.0, None, Op.is_lt)
+    ts(["jm"], ["q15"], T.q15[:, :], T.jm[:, :], 15.0, None, Op.is_equal)
+    op("g", ["n15"], ["sh1"], lambda e: e.affine_select(T.sh1[:, :], T.n15[:, :], [[-1, 128]], Op.is_equal, 0.0, -1, 1))
+    op("g", ["q15"], ["sh15"], lambda e: e.affine_select(T.sh15[:, :], T.q15[:, :], [[-1, 128]], Op.is_equal, 0.0, 15, 1))
+    copy("v", IOT + ["xu"], ["xaf"], T.xaf[:, :], T.iot[:, :].indirect(T.xu[:, 0:16]))
+    ts(["em", "pf"], ["e8"], T.e8[:, :], T.em[:, :], T.pf[0:8, 0:1], None, Op.is_equal)
+    ts(["xk"], ["e1"], T.e1[:, :], T.xk[:, :], 7.0, None, Op.mult)
+    ts(["xq"], ["e2"], T.e2[:, :], T.xq[:, :], -0.75, None, Op.mult)
+    ts(["trb", "pq45"], ["tr"], T.tr[:, :], T.trb[:, :], T.pq[:, 4:5], None, Op.add)
+    fill("s1e", T.same1[:, 0:1], 0.0)
+    mm(["e8", "v8"], ["P1"], PS[1][:, 0:256], T.e8[:, :], T.v8[:, :])
+    shifted(T.xf1, ["xf1", "xf1e"], 2)
+    copy("s", ["P1"], ["vf"], T.vf[:, :], PS[1][:, 0:256])
+    tt(["e1", "xi"], ["e1"], T.e1[:, :], T.e1[:, :], T.xi[:, 16:48], Op.add)
+    tt(["xaf"], ["same1"], T.same1[:, 1:256], T.xaf[:, 1:256], T.xaf[:, 0:255], Op.is_equal)
+    tt(["e1", "e2"], ["e1"], T.e1[:, :], T.e1[:, :], T.e2[:, :], Op.add)
+    ends(T.xf1, ["xf1", "xf1e"], "of1", 2, (
+        lambda: copy("v", ["e1"], ["obc"], T.obc[:, :], T.e1[:, :]),
+        lambda: copy("v", ["a16"], ["a16b"], T.a16[:, 128:256], T.a16[:, 0:128]),
+        lambda: ts(["iot0", "pf"], ["ident"], T.ident[:, :], T.iot[:, 0:128], pf, None, Op.is_equal)))
+
+    L1 = ["in1", "own1"]
+
+    def spread(k, bank, a, b):
+        mm(L1 + [SEL[k]], ["P%d" % bank], PS[bank][:, 0:b - a], T.selb[:, 128 * k:128 * k + 128], T.land1[:, a:b])
+
+    for k in (4, 5, 6, 7, 0, 1):
+        spread(k, k, 0, 512)
+    spread(3, 3, 0, 256)
+    spread(2, 2, 0, 512)
+    for k in (4, 5, 6, 7):
+        copy("vs"[k % 2], ["P%d" % k], ["wc%d" % k], T.wc[:, 512 * k - 2048:512 * k - 1536], PS[k][:, :])
+    spread(3, 4, 256, 512)
+
+    def window_b(q, k, lo, n, bank):
+        copy(q, ["P%d" % bank], ["wb%d" % k], T.wb[:, lo:lo + n], PS[bank][:, 0:n])
+
+    window_b("s", 1, 512, 512, 1)
+    window_b("v", 0, 0, 512, 0)
+    tt(["wc4", "wc5", "wc6", "wc7", "obc", "vf"], ["w"], T.w[:, :], T.wc[:, :].indirect(T.obc[:, 16:32]), T.vf[:, :], Op.mult)
+    window_b("s", 2, 1024, 512, 2)
+    window_b("v", 3, 1536, 256, 3)
+    window_b("s", 4, 1792, 256, 4)
+    WB = ["wb%d" % k for k in range(5)]
+    tt(WB + ["obc", "w"], ["p1"], T.p1[:, :], T.wb[:, :].indirect(T.obc[:, 0:16]), T.w[:, :], Op.mult)
+    copy("s", IOT + ["xu"], ["xbf"], T.xbf[:, :], T.iot[:, :].indirect(T.xu[:, 16:32]))
+    copy("s", ["xaf", "xu"], ["xa2"], T.xa2[:, :], T.xaf[:, :].indirect(T.xu[:, 48:64]))
+    copy("s", ["xbf", "xu"], ["xb2"], T.xb2[:, :], T.xbf[:, :].indirect(T.xu[:, 48:64]))
+    zero("win2")
+
+    def slab_sums(p, pk, c, same, keys, win, of):
+        op("v", [pk] + keys, [c], lambda e: e.tensor_tensor_scan(T[c][:, :], same[:, :], p, 0.0, Op.mult, Op.add))
+        copy("v", [c, of], [win], T[win][:, :].indirect(T[of][:, :]), T[c][:, :])
+
+    def add_groups(bank, out, data, keys):
+        mm(keys + ["a16"], ["P%d" % bank], out, data, T.a16[:, 0:16])
+
+    def block(i, b):
+        return i // 4, PS[i // 4][:, 32 * (i % 4) + b:32 * (i % 4) + 32:2]
+
+    def to_owners(x, win, sb, land, between):
+        for i, q in enumerate(turn):
+            for b in range(2):
+                bank, out = block(i, b)
+                add_groups(bank, out, T[win][:, 256 * q + 128 * b:256 * q + 128 * b + 128], [win])
+        for h in range(2):
+            between[h]()
+            copy("v", ["P%d" % h], [sb + "ab"[h]], T[sb][:, 128 * h:128 * h + 128], PS[h][:, 0:128])
+            send(x, h, 32, [sb + "ab"[h]], T[sb], land)
+
+    def turn_back(x, land, r, at=0):
+        for b in range(2):
+            transpose(["in%d" % x, "own%d" % x], ["P%d" % (2 + b)], PS[2 + b][:, 0:128], land[:, b::2])
+            copy("vs"[b], ["P%d" % (2 + b)], [r + "ab"[b]], T[r][:, at + 128 * b:at + 128 * b + 128], PS[2 + b][:, 0:128])
+
+    def own_columns(r, win, lo):
+        copy("v", [r + "a", r + "b", "lu", win], [win], T[win][:, 0:2048].indirect(T.lu[:, lo:lo + 16]), T[r][:, :])
+
+    def gather_all(win, keys, lists, lkey, gb, place):
+        for k in range(8):
+            copy("vs"[k % 2], keys + [lkey], ["%s%d" % (gb, k)], T[gb][:, 256 * k:256 * k + 256],
+                 win.indirect(lists[:, 16 * k:16 * k + 16]))
+            for b in range(2):
+                bank, out = place(k, b)
+                add_groups(bank, out, T[gb][:, 256 * k + 128 * b:256 * k + 128 * b + 128], ["%s%d" % (gb, k)])
+
+    DIAG = (("b", "xb2", "xf2"), ("a", "xa2", "xd"))
+
+    def masked():
+        for c, src, out in DIAG:
+            tt([src, "a16", "a16b"], ["d%s0" % c], T["d%s0" % c][:, :], T[src][:, :], T.a16[:, :], Op.mult)
+
+    slab_sums(T.p1[:, :], "p1", "c1", T.same1, ["same1", "s1e"], "win1", "of1")
+    to_owners(2, "win1", "sb2", T.land2, (
+        lambda: tt(["xb2"], ["same2"], T.same2[:, 1:256], T.xb2[:, 1:256], T.xb2[:, 0:255], Op.is_equal), masked))
+    for i, r in enumerate(turn):
+        to_groups(["lhb", "llb"], 4, 16 * i, 16, r, T.lhb[:, 32:48], T.llb[:, 32:48])
+    copy("v", ["li"], ["lu"], T.lu[:, :], T.li[:, :])
+    copy("s", ["w", "xu"], ["w2"], T.w2[:, :], T.w[:, :].indirect(T.xu[:, 48:64]))
+    for n in range(1, 5):
+        for c, src, out in DIAG:
+            s = T["d%s%d" % (c, n - 1)]
+            dst, key = (T["d%s%d" % (c, n)][:, :], "d%s%d" % (c, n)) if n < 4 else (T[out][:, 0:16], out)
+            tt(["d%s%d" % (c, n - 1)], [key], dst, s[:, 0::2], s[:, 1::2], Op.add)
+        if n == 1:
+            fill("xf2e", T.xf2[:, 16:24], -1.0)
+        elif n == 2:
+            copy("v", ["P4"], ["lau"], T.lau[:, :], PS[4][:, 0:128])
+        elif n == 3:
+            fill("s2e", T.same2[:, 0:1], 0.0)
+            fill("r3e", T.r3[:, 0:8], 0.0)
+    copy("s", ["fa", "lu"], ["fag"], T.fag[:, :], T.far[:, :].indirect(T.lu[:, 32:48]))
+    for b in range(2):
+        transpose(["w2"], ["P5"], PS[5][:, 128 * b:128 * b + 128], T.w2[:, 128 * b:128 * b + 128])
+    shifted(T.xf2, ["xf2", "xf2e"], 6)
+    copy("s", ["P5"], ["w2t"], T.w2t[:, :], PS[5][:, 0:256])
+    for b in range(2):
+        transpose(["fag"], ["P7"], PS[7][:, 128 * b:128 * b + 128], T.fag[:, 128 * b:128 * b + 128])
+    FAT = []
+    for b in range(2):
+        for a, n, i in ((me + 1, n_ranks - 1 - me, 0), (0, me + 1, n_ranks - 1 - me)):
+            if n:
+                FAT.append("fat%d%d" % (b, a))
+                copy("s", ["P7"], [FAT[-1]], T.fat[:, 32 * i + b:32 * (i + n):2],
+                     PS[7][:, 128 * b + 16 * a:128 * b + 16 * (a + n)])
+    ends(T.xf2, ["xf2", "xf2e"], "of2", 6, (
+        lambda: copy("v", ["xd"], ["ahb"], T.ahb[:, :], T.xd[:, :]),
+        lambda: tt(["xd", "ahb"], ["alb"], T.alb[:, :], T.xd[:, :], T.ahb[:, :], Op.subtract),
+        lambda: (fill("r3f", T.r3[:, 264:272], 0.0),
+                 ts(["pq45"], ["pq6"], T.pq[:, 6:7], T.pq[:, 5:6], 256.0, -8.0, Op.mult, Op.add))))
+    turn_back(2, T.land2, "r2")
+    for r in range(8):
+        to_groups(["ahb", "alb"], 4, 16 * r, 16, r, T.ahb[:, :], T.alb[:, :])
+    own_columns("r2", "win2", 32)
+    gather_all(T.win2[:, :], ["win2"], T.lau, "lau", "gb2", block)
+    for h in range(2):
+        tt(["P%d" % h] + FAT, ["sb3" + "ab"[h]], T.sb3[:, 128 * h:128 * h + 128], PS[h][:, 0:128],
+           T.fat[:, 128 * h:128 * h + 128], Op.mult)
+        send(3, h, 32, ["sb3" + "ab"[h]], T.sb3, T.land3)
+    zero("win3")
+    ts(["P4", "pq6"], ["cu"], T.cu[:, :], PS[4][:, 0:128], T.pq[:, 6:7], 7.0, Op.subtract, Op.max)
+    ts(["cu"], ["l3"], T.l3[:, :], T.cu[:, :], 264.0, None, Op.min)
+
+    def rows_part(win, bank, blocks):
+        for blk in blocks:
+            add_groups(bank, PS[bank][:, blk:256:16], T[win][:, 128 * blk:128 * blk + 128], [win])
+
+    rows_part("win2", 7, range(8))
+    turn_back(3, T.land3, "r3", 8)
+    gather_all(T.r3[:, :], ["r3a", "r3b", "r3e", "r3f"], T.l3, "l3", "gb3",
+               lambda k, b: (b, PS[b][:, 16 * k:16 * k + 16]))
+    for b in range(2):
+        tt(["P%d" % b, "w2t"], ["pt%d" % b], T.pt[:, 128 * b:128 * b + 128], PS[b][:, 0:128],
+           T.w2t[:, 128 * b:128 * b + 128], Op.mult)
+    for b in range(2):
+        transpose(["pt%d" % b], ["P4"], PS[4][:, 128 * b:128 * b + 128], T.pt[:, 128 * b:128 * b + 128])
+    slab_sums(PS[4][:, 0:256], "P4", "c2", T.same2, ["same2", "s2e"], "win3", "of2")
+    to_owners(4, "win3", "sb4", T.land4, (lambda: zero("win4"), lambda: None))
+    rows_part("win2", 7, range(8, 16))
+    for h in range(2):
+        copy("v", ["P7"], ["ta%d" % h], T.ta[:, 128 * h:128 * h + 128], PS[7][:, 128 * h:128 * h + 128])
+        transpose(["ta%d" % h], ["P%d" % (5 + h)], PS[5 + h][:, 0:128], T.ta[:, 128 * h:128 * h + 128])
+    for h in range(2):
+        tt(["P%d" % (5 + h), "fa2"], ["ya%d" % h], T["ya%d" % h][:, :], PS[5 + h][:, 0:128],
+           T.fa2[:, 128 * h:128 * h + 128], Op.mult)
+        dma("y", "do", ["ya%d" % h], None, T.ya[8 * h:8 * h + 8, :], T["ya%d" % h][:, :])
+    turn_back(4, T.land4, "r4")
+    own_columns("r4", "win4", 0)
+    rows_part("win4", 4, range(16))
+    for h in range(2):
+        copy("v", ["P4"], ["tb%d" % h], T.tb[:, 128 * h:128 * h + 128], PS[4][:, 128 * h:128 * h + 128])
+        transpose(["tb%d" % h], ["P%d" % (5 + h)], PS[5 + h][:, 0:128], T.tb[:, 128 * h:128 * h + 128])
+    for h in range(2):
+        copy("sv"[h], ["P%d" % (5 + h)], ["yb%d" % h], T["yb%d" % h][:, :], PS[5 + h][:, 0:128])
+        dma("sy"[h], "do", ["yb%d" % h], None, T.yb[8 * h:8 * h + 8, :], T["yb%d" % h][:, :])
+    for name in sorted(count):
+        g.wait_ge(T.sem[name], count[name])

@@ -1,55 +1,58 @@
-import numpy as np
 from concourse.bass import DstId, RemoteDMATransfer
 from concourse.mybir import AluOpType, ActivationFunctionType
 
-F32, BF, I32, U16 = "float32", "bfloat16", "int32", "uint16"
+F32, BF, F16, I32, U16 = "float32", "bfloat16", "float16", "int32", "uint16"
+CUT1 = 10
+PARTS3 = ((0, 4), (4, 8))
 SCRATCH = {
     "pi": ("sbuf", [128, 8], I32), "pm": ("sbuf", [128, 8], I32), "pf": ("sbuf", [128, 8], F32),
-    "pq": ("sbuf", [128, 8], F32), "ofc": ("sbuf", [128, 8], F32), "ofu": ("sbuf", [128, 8], U16),
-    "jm": ("sbuf", [128, 128], F32), "k8": ("sbuf", [128, 8], F32), "m8": ("sbuf", [128, 8], F32),
+    "pq": ("sbuf", [128, 16], F32), "ofu": ("sbuf", [128, 8], U16), "pick": ("sbuf", [128, 8], U16),
+    "jm": ("sbuf", [128, 128], BF), "idx": ("sbuf", [128, 128], BF), "j32": ("sbuf", [128, 160], BF),
+    "su": ("sbuf", [128, 256], F16), "z32": ("sbuf", [128, 128], F16), "wsel": ("sbuf", [128, 240], BF),
+    "a16": ("sbuf", [128, 16], F32), "a32": ("sbuf", [128, 32], F32),
     "em": ("sbuf", [8, 128], F32), "e8": ("sbuf", [8, 128], F32),
-    "iot": ("sbuf", [128, 2048], F32), "a16": ("sbuf", [128, 256], F32),
-    "selb": ("sbuf", [128, 1024], BF), "ident": ("sbuf", [128, 128], F32),
+    "iot": ("sbuf", [128, 2048], F32), "ident": ("sbuf", [128, 128], F32),
     "q15": ("sbuf", [128, 128], F32), "n15": ("sbuf", [128, 128], F32),
     "sh1": ("sbuf", [128, 128], F32), "sh15": ("sbuf", [128, 128], F32),
     "trb": ("sbuf", [128, 16], F32), "tr": ("sbuf", [128, 16], F32),
-    "li": ("sbuf", [128, 48], I32), "xi": ("sbuf", [128, 64], I32), "v8": ("sbuf", [8, 256], F32),
+    "dpb": ("sbuf", [128, 8], F32), "dpo": ("sbuf", [128, 8], U16),
+    "li": ("sbuf", [128, 32], I32), "lai": ("sbuf", [128, 32], I32), "xi": ("sbuf", [128, 64], I32),
+    "v8": ("sbuf", [8, 256], F32),
     "fbc": ("sbuf", [128, 2048], BF), "far": ("sbuf", [128, 2048], BF), "fa2": ("sbuf", [128, 256], BF),
-    "lhb": ("sbuf", [128, 48], BF), "llb": ("sbuf", [128, 48], BF),
-    "rep": ("sbuf", [128, 256], F32), "lau": ("sbuf", [128, 128], U16),
-    "lt": ("sbuf", [128, 32], U16), "lu": ("sbuf", [128, 48], U16), "xu": ("sbuf", [128, 64], U16),
-    "xk": ("sbuf", [128, 32], I32), "xq": ("sbuf", [128, 32], I32),
-    "e1": ("sbuf", [128, 32], F32), "e2": ("sbuf", [128, 32], F32), "obc": ("sbuf", [128, 32], U16),
-    "ahb": ("sbuf", [128, 16], BF), "alb": ("sbuf", [128, 16], BF),
-    "cu": ("sbuf", [128, 128], F32), "l3": ("sbuf", [128, 128], U16),
-    "xaf": ("sbuf", [128, 256], F32), "xbf": ("sbuf", [128, 256], F32),
-    "xa2": ("sbuf", [128, 256], F32), "xb2": ("sbuf", [128, 256], F32),
-    "same1": ("sbuf", [128, 256], F32), "same2": ("sbuf", [128, 256], F32),
-    "xf1": ("sbuf", [128, 24], F32), "xf2": ("sbuf", [128, 24], F32), "xd": ("sbuf", [128, 16], F32),
+    "lh": ("sbuf", [128, 32], F16), "rep": ("sbuf", [128, 256], F32), "lt": ("sbuf", [128, 32], U16),
+    "xk": ("sbuf", [128, 48], I32), "xq": ("sbuf", [128, 48], I32),
+    "e1": ("sbuf", [128, 48], F32), "e2": ("sbuf", [128, 48], F32), "xh": ("sbuf", [128, 32], F16),
+    "cu1": ("sbuf", [128, 128], F32), "l1": ("sbuf", [128, 128], U16),
+    "xu": ("sbuf", [128, 48], U16), "ob2": ("sbuf", [128, 32], U16),
+    "lk": ("sbuf", [128, 32], I32), "lq": ("sbuf", [128, 32], I32),
+    "f1": ("sbuf", [128, 32], F32), "f2": ("sbuf", [128, 32], F32),
+    "lau0": ("sbuf", [128, 16], U16), "lp": ("sbuf", [128, 32], U16), "lph": ("sbuf", [128, 16], F16),
+    "lau": ("sbuf", [128, 128], U16),
+    "xx": ("sbuf", [128, 512], F32), "ex": ("sbuf", [128, 512], F32), "xt": ("sbuf", [128, 512], F32),
+    "xah": ("sbuf", [128, 16], F16), "cu3": ("sbuf", [128, 64], F32), "l3": ("sbuf", [128, 64], U16),
+    "same": ("sbuf", [128, 544], F32),
+    "xf1": ("sbuf", [128, 24], F32), "xf2": ("sbuf", [128, 40], F32),
     "of1": ("sbuf", [128, 16], U16), "of2": ("sbuf", [128, 16], U16),
-    "nq": ("sbuf", [128, 16], F32), "td": ("sbuf", [128, 16], F32),
-    "da0": ("sbuf", [128, 256], F32), "da1": ("sbuf", [128, 128], F32), "da2": ("sbuf", [128, 64], F32),
-    "da3": ("sbuf", [128, 32], F32),
-    "db0": ("sbuf", [128, 256], F32), "db1": ("sbuf", [128, 128], F32), "db2": ("sbuf", [128, 64], F32),
-    "db3": ("sbuf", [128, 32], F32),
-    "vf": ("sbuf", [128, 256], F32), "sb1": ("sbuf", [128, 512], BF), "land1": ("sbuf", [128, 512], BF),
-    "wb": ("sbuf", [128, 2048], BF), "wc": ("sbuf", [128, 2048], BF),
+    "eq1": ("sbuf", [128, 16], F32), "eq2": ("sbuf", [128, 16], F32),
+    "nu1": ("sbuf", [128, 16], U16), "nu2": ("sbuf", [128, 16], U16), "td": ("sbuf", [128, 16], F32),
+    "vf": ("sbuf", [128, 256], F32), "sb1": ("sbuf", [128, 448], BF), "land1": ("sbuf", [128, 544], BF),
+    "gb1": ("sbuf", [128, 2048], BF),
     "w": ("sbuf", [128, 256], F32), "w2": ("sbuf", [128, 256], F32), "w2t": ("sbuf", [128, 256], F32),
     "p1": ("sbuf", [128, 256], F32), "c1": ("sbuf", [128, 256], F32),
     "win1": ("sbuf", [128, 2304], F32), "win2": ("sbuf", [128, 2048], F32),
     "win3": ("sbuf", [128, 2304], F32), "win4": ("sbuf", [128, 2048], F32),
     "sb2": ("sbuf", [128, 256], F32), "land2": ("sbuf", [128, 256], F32), "r2": ("sbuf", [128, 256], F32),
     "fag": ("sbuf", [128, 256], F32), "fat": ("sbuf", [128, 256], F32), "gb2": ("sbuf", [128, 2048], F32),
-    "sb3": ("sbuf", [128, 256], F32), "land3": ("sbuf", [128, 256], F32), "r3": ("sbuf", [128, 272], F32),
-    "gb3": ("sbuf", [128, 2048], F32), "pt": ("sbuf", [128, 256], F32), "c2": ("sbuf", [128, 256], F32),
+    "sb3": ("sbuf", [128, 256], F32), "land3": ("sbuf", [128, 256], F32), "dup3": ("sbuf", [128, 512], F32),
+    "r3": ("sbuf", [128, 528], F32), "gb3": ("sbuf", [128, 1024], F32),
+    "pt": ("sbuf", [128, 256], F32), "p2": ("sbuf", [128, 256], F32), "c2": ("sbuf", [128, 256], F32),
     "sb4": ("sbuf", [128, 256], F32), "land4": ("sbuf", [128, 256], F32), "r4": ("sbuf", [128, 256], F32),
-    "ta": ("sbuf", [128, 256], F32), "ya0": ("sbuf", [128, 128], F32), "ya1": ("sbuf", [128, 128], F32),
-    "tb": ("sbuf", [128, 256], F32), "yb0": ("sbuf", [128, 128], F32), "yb1": ("sbuf", [128, 128], F32),
+    "ta": ("sbuf", [128, 256], F32), "yas": ("sbuf", [128, 256], F32), "ybs": ("sbuf", [128, 256], F32),
 }
 for _b in range(8):
     SCRATCH["ps%d" % _b] = ("psum", [128, 512], F32)
-SEMAPHORES = ["qg", "qv", "qs", "qt", "dl", "db", "dc", "dx", "dv", "da", "df", "do",
-              "arr1", "arr2", "arr3", "arr4", "sent"]
+SEMAPHORES = ["qg", "qv", "qs", "qt", "dl", "db", "dc", "dx", "dv", "da", "df", "dm", "do",
+              "arr1", "arr2", "arr30", "arr31", "arr32", "arr33", "arr4", "sent1", "sent"]
 
 
 def rank_program(g, core, T, topo):
@@ -59,10 +62,11 @@ def rank_program(g, core, T, topo):
     cores = T.cores
     n_ranks = len(cores)
     Op = AluOpType
-    COPY, IDENT = ActivationFunctionType.Copy, ActivationFunctionType.Identity
+    COPY, RELU = ActivationFunctionType.Copy, ActivationFunctionType.Relu
     Q = {"g": g, "v": g.vector, "s": g.scalar, "t": g.tensor, "y": g.sync}
     count, known, snap, written, readers = {}, {q: {} for q in Q}, {}, {}, {}
-    turn = [(me + 1 + i) % n_ranks for i in range(n_ranks)]
+    turn = [me ^ j for j in sorted(range(1, n_ranks), key=lambda j: (topo.mates(core, cores[me ^ j]), j))]
+    CALLS = [sorted(turn[a:a + 2]) for a in range(0, n_ranks - 1, 2)]
 
     def learn(q, tok):
         name, n = tok
@@ -79,10 +83,11 @@ def rank_program(g, core, T, topo):
                 learn(q, tok)
 
     def before(q, reads, writes):
-        toks = [written[k] for k in reads if k in written]
+        toks = [written[k] for k in reads]
         for k in writes:
             if k in written and not (q == "t" and written[k][0] == "qt"):
                 toks.append(written[k])
+        for k in writes + [k for k in reads if k[0] == "P"]:
             toks += [t for t in readers.get(k, []) if t[0] != "q" + q]
         need(q, toks)
 
@@ -127,313 +132,410 @@ def rank_program(g, core, T, topo):
     def fill(key, out, c):
         op("v", [], [key], lambda e: e.memset(out, c))
 
-    def mm(reads, writes, out, lhs, rhs, start=True, stop=True):
-        op("t", reads, writes, lambda e: e.matmul(out, lhs, rhs, start, stop))
+    tile = {}
 
-    def transpose(reads, writes, out, in_):
-        op("t", reads + ["ident"], writes, lambda e: e.transpose(out, in_, T.ident[:, :]))
+    def tensor(reads, bank, rows, fn):
+        key = "P%d" % bank
+        if key in written and tile.get(key) != rows:
+            need("t", [written[key]])
+        tile[key] = rows
+        op("t", reads, [key], fn)
 
-    def zero(win):
-        op("s", IOT, [win], lambda e: e.activation(T[win][:, 0:2048], T.iot[:, 0:2048], COPY, scale=0.0))
+    def mm(reads, bank, out, lhs, rhs, start=True, stop=True, rows=None):
+        tensor(reads, bank, rows, lambda e: e.matmul(out, lhs, rhs, start, stop))
 
-    def send(x, half, width, reads, src, land):
+    def transpose(reads, bank, out, in_):
+        tensor(reads + ["ident"], bank, None, lambda e: e.transpose(out, in_, T.ident[:, :]))
+
+    def blocks_turned(reads, writes, out, in_):
+        op("v", reads, writes, lambda e: e.transpose(out, in_))
+
+    def iota(key, out, pattern, base, per_row=0):
+        op("g", [], [key], lambda e: e.iota(out, pattern, base, per_row, allow_small_or_imprecise_dtypes=True))
+
+    def zero(win, a, b, reads=("fb", "fc"), src=None):
+        key = "%s@%d" % (win, a)
+        op("s", list(reads), [key], lambda e: e.activation(T[win][:, a:b], src or T.fbc[:, a:b], COPY, scale=0.0))
+        return key
+
+    def send(arr, sent, dests, reads, src, land):
         before("g", reads, [])
         trs = []
-        for i in ((0, 1, 2, 3), (4, 5, 6))[half]:
-            d = cores[turn[i]]
-            rid, pid = topo.addr(d, core)
-            eng = topo.engines(core, d)[2 * (i % 4):2 * (i % 4) + 2]
+        for i, r in enumerate(dests):
+            rid, pid = topo.addr(cores[r], core)
+            eng = topo.engines(core, cores[r])
+            n = 1 << ((len(eng) // len(dests)).bit_length() - 1)
             trs.append(RemoteDMATransfer(
-                dst_ids=[DstId(rid=rid, pnc=pid)], dma_engine_mask=sum(1 << e for e in eng), remote_sem=T.sem["arr%d" % x],
-                srcs=[src[:, i * width:(i + 1) * width]], dsts=[land[:, me * width:(me + 1) * width]], alu_op=0))
-        g.remote_dma_fused(trs, local_sem=T.sem.sent)
-        count["sent"] = count.get("sent", 0) + 2 * len(trs)
-        if half:
-            count["arr%d" % x] = 2 * (n_ranks - 1)
-            written["in%d" % x] = ("arr%d" % x, 2 * (n_ranks - 1))
-            copy("v", reads, ["own%d" % x], land[:, me * width:(me + 1) * width], src[:, 7 * width:8 * width])
+                dst_ids=[DstId(rid=rid, pnc=pid)], dma_engine_mask=sum(1 << e for e in eng[n * i:n * i + n]),
+                remote_sem=T.sem[arr], srcs=[src(i, r)], dsts=[land], alu_op=0))
+            for name in (arr, sent):
+                count[name] = count.get(name, 0) + n
+        g.remote_dma_fused(trs, local_sem=T.sem[sent])
+        written[arr] = (arr, count[arr])
+        written[sent] = (sent, count[sent])
+
+    def in_turns(*chains):
+        for k in range(max(len(c) for c in chains)):
+            for c in chains:
+                if k < len(c):
+                    c[k]()
 
     PS = [T["ps%d" % b] for b in range(8)]
 
     dma("y", "dl", [], "li", T.li[:, 0:16], T.lb[:, :])
     dma("s", "dl", [], "li", T.li[:, 16:32], T.lc[:, :])
-    dma("y", "dl", [], "li", T.li[:, 32:48], T.la[:, :])
     for k in range(4):
         dma("y", "db", [], "fb", T.fbc[16 * k:16 * k + 16, :], T.fb[:, :])
         dma("s", "dc", [], "fc", T.fbc[64 + 16 * k:80 + 16 * k, :], T.fc[:, :])
-    dma("y", "dx", [], "xi", T.xi[:, 0:16], T.xa[:, :])
-    dma("s", "dx", [], "xi", T.xi[:, 16:32], T.xb[:, :])
-    dma("y", "dx", [], "xi", T.xi[:, 32:48], T.xc[:, :])
-    dma("y", "dx", [], "xi", T.xi[:, 48:64], T.ob[:, :])
+    for k, x in enumerate((T.xa, T.xc, T.xb, T.ob)):
+        dma("y", "dx", [], "xi", T.xi[:, 16 * k:16 * k + 16], x[:, :])
     dma("y", "dv", [], "v8", T.v8[:, :], T.v[:, :])
-    for k in range(8):
-        dma("y", "da", [], "fa", T.far[16 * k:16 * k + 16, :], T.fa[:, :])
-    for h in range(2):
-        dma("y", "df", [], "fa2", T.fa2[:, 128 * h:128 * h + 128], T.fa[8 * h:8 * h + 8, :])
+    dma("y", "dm", [], "lai", T.lai[:, 0:16], T.la[:, :])
+    dma("y", "dm", [], "lai", T.lai[:, 16:32], T.lb[:, :])
 
-    fl = {"allow_small_or_imprecise_dtypes": True}
     op("g", [], ["pi"], lambda e: e.iota(T.pi[:, 0:1], [[0, 1]], 0, 1))
-    op("g", [], ["k8"], lambda e: e.iota(T.k8[:, :], [[1, 8]], 0, 0, **fl))
-    op("g", [], ["jm"], lambda e: e.iota(T.jm[:, :], [[0, 8], [1, 16]], 0, 0, **fl))
-    op("g", [], ["iot0"], lambda e: e.iota(T.iot[:, 0:256], [[1, 256]], 0, 0, **fl))
-    op("g", [], ["iot1024"], lambda e: e.iota(T.iot[:, 1024:2048], [[1, 1024]], 1024, 0, **fl))
+    iota("jm", T.jm[:, :], [[0, 8], [1, 16]], 0)
+    iota("pf", T.pf[:, 0:1], [[0, 1]], 0, 1)
+    iota("l1a", T.land1[:, 0:16], [[0, 16]], 0)
+    iota("l1b", T.land1[:, 528:544], [[0, 16]], 0)
+    iota("idx", T.idx[:, :], [[1, 128]], 0)
+    iota("em", T.em[:, :], [[1, 8], [0, 16]], 0, -1)
+    iota("trb", T.trb[:, :], [[16, 16]], 2048)
     pf = T.pf[:, 0:1]
+    W1 = [zero("win1", 0, 128, ["jm"], T.jm[:, :])]
+    for a, b in ((128, 256), (256, 512), (512, 1024), (1024, 1536)):
+        W1.append(zero("win1", a, b, list(W1), T.win1[:, 0:b - a]))
 
     def bits(j, m):
         ts(["pi"], ["pm%d" % j], T.pm[:, j:j + 1], T.pi[:, 0:1], m, None, Op.bitwise_and)
 
-    bits(4, 15)
-    ts(["pi"], ["pm5"], T.pm[:, 5:6], T.pi[:, 0:1], 4, None, Op.logical_shift_right)
-    copy("v", ["pi"], ["pf"], pf, T.pi[:, 0:1])
-    copy("v", ["pm4", "pm5"], ["pq45"], T.pq[:, 4:6], T.pm[:, 4:6])
-    bits(0, 12)
-    bits(2, 240)
-    ts(["k8", "pq45"], ["m8"], T.m8[:, :], T.k8[:, :], T.pq[:, 5:6], None, Op.is_equal)
-    ts(["jm", "pq45"], ["a16"], T.a16[:, 0:128], T.jm[:, :], T.pq[:, 4:5], None, Op.is_equal)
-    ts(["pm2", "pf"], ["pq0"], T.pq[:, 0:1], T.pm[:, 2:3], -0.75, pf, Op.mult, Op.add)
-    for k in range(8):
-        if k % 2:
-            op("s", ["a16", "m8"], ["sel%d" % k], lambda e, k=k: e.activation(
-                T.selb[:, 128 * k:128 * k + 128], T.a16[:, 0:128], COPY, scale=T.m8[:, k:k + 1]))
-        else:
-            ts(["a16", "m8"], ["sel%d" % k], T.selb[:, 128 * k:128 * k + 128], T.a16[:, 0:128], T.m8[:, k:k + 1],
-               None, Op.mult)
-        if k == 2:
-            ts(["pm0", "pq0"], ["ofc"], T.ofc[:, 0:1], T.pm[:, 0:1], 7.0, T.pq[:, 0:1], Op.mult, Op.add)
-        if k == 6:
-            copy("v", ["ofc"], ["ofu"], T.ofu[:, 0:1], T.ofc[:, 0:1])
-    SEL = ["sel%d" % k for k in range(8)]
-    for a, b in ((256, 512), (512, 1024)):
-        op("s", ["iot0", "iot%d" % (a // 2)], ["iot%d" % a],
-           lambda e, a=a, b=b: e.activation(T.iot[:, a:b], T.iot[:, 0:b - a], IDENT, bias=float(a)))
-    IOT = ["iot0", "iot256", "iot512", "iot1024"]
+    def col(j):
+        return T.pq[:, j:j + 1]
 
-    def to_groups(reads, bank, col, n, r, hi, lo):
-        out = PS[bank][:, col:col + n]
-        mm(reads + [SEL[r]], ["P%d" % bank], out, T.selb[:, 128 * r:128 * r + 128], hi, True, False)
-        mm(reads + [SEL[r]], ["P%d" % bank], out, T.selb[:, 128 * r:128 * r + 128], lo, False, True)
+    def more(j, factor, key, out, okey, last):
+        ts(["pm%d" % j, key], [okey], out, T.pm[:, j:j + 1], factor, last, Op.mult, Op.add)
 
-    copy("v", ["li"], ["lhb"], T.lhb[:, :], T.li[:, :])
-    tt(["li", "lhb"], ["llb"], T.llb[:, :], T.li[:, :], T.lhb[:, :], Op.subtract)
-    for i, r in enumerate(turn):
-        to_groups(["lhb", "llb"], 2 * (i // 4), 32 * (i % 4), 32, r, T.lhb[:, 0:32], T.llb[:, 0:32])
+    bits(0, 31)
+    bits(2, 2)
+    copy("v", ["pm0"], ["p31"], col(0), T.pm[:, 0:1])
+    bits(3, 12)
+    ts(["jm", "p31"], ["su0"], T.su[:, 0:128], T.jm[:, :], col(0), None, Op.is_equal)
+    bits(4, 48)
+    ts(["jm", "p31"], ["su1"], T.su[:, 128:256], T.jm[:, :], 16.0, col(0), Op.add, Op.is_equal)
+    more(2, 3.0, "pf", col(2), "o1", pf)
+    bits(5, 64)
+    more(3, 7.0, "o1", col(10), "o2", col(2))
+    bits(1, 15)
+    more(4, -0.875, "o2", col(2), "o3", col(10))
 
-    def deal(h):
+    def to_groups(reads, bank, out, r, table):
+        rows = slice(32 * (r // 2), 32 * (r // 2) + 32)
+        mm(reads + ["su%d" % (r % 2)], bank, out, T.su[rows, 128 * (r % 2):128 * (r % 2) + 128], table(rows), rows=rows)
+
+    copy("v", ["li"], ["lh"], T.lh[:, :], T.li[:, :])
+    more(5, -0.75, "o3", T.ofu[:, 0:1], "ofu", col(2))
+    copy("v", ["pm1"], ["p15"], col(1), T.pm[:, 1:2])
+    for i, r in enumerate(turn + [me]):
+        to_groups(["lh"], i // 4, PS[i // 4][:, 32 * (i % 4):32 * (i % 4) + 32], r, lambda rows: T.lh[rows, :])
+    for h in range(2):
+        copy("v", ["P%d" % h], ["rep%d" % h], T.rep[:, 128 * h:128 * h + 128], PS[h][:, 0:128])
+    for h in range(2):
         copy("v", ["rep%d" % h, "ofu"], ["lt%d" % h], T["lt"][:, 16 * h:16 * h + 16],
              T.rep[:, 128 * h:128 * h + 128].indirect(T.ofu[:, 0:1]))
-
-    def columns(h):
-        for q, a in (("v", 16 * h), ("s", 16 * h + 8)):
-            copy(q, ["fb", "fc", "lt%d" % h], ["sb1%s%d" % (q, h)], T.sb1[:, 16 * a:16 * a + 128],
-                 T.fbc[:, :].indirect(T["lt"][:, a:a + 8]))
-
-    copy("v", ["P0"], ["rep0"], T.rep[:, 0:128], PS[0][:, 0:128])
-    deal(0)
-    copy("v", ["P2"], ["rep1"], T.rep[:, 128:256], PS[2][:, 0:128])
-    columns(0)
-    send(1, 0, 64, ["sb1v0", "sb1s0"], T.sb1, T.land1)
-    deal(1)
-    columns(1)
-    send(1, 1, 64, ["sb1v1", "sb1s1"], T.sb1, T.land1)
-
-    op("g", [], ["em"], lambda e: e.iota(T.em[:, :], [[1, 8], [0, 16]], 0, 0, **fl))
-    op("g", [], ["trb"], lambda e: e.iota(T.trb[:, :], [[16, 16]], 2048, 0, **fl))
-    zero("win1")
-
-    def shifted(xf, keys, bank):
-        mm(keys + ["sh1"], ["P%d" % bank], PS[bank][:, 0:16], T.sh1[:, :], xf[:, 0:16], True, False)
-        mm(keys + ["sh15"], ["P%d" % bank], PS[bank][:, 0:16], T.sh15[:, :], xf[:, 1:17], False, True)
-
-    def ends(xf, keys, of, bank, between):
-        a, b, c = between
-        tt(keys + ["tr"], ["td"], T.td[:, :], xf[:, 0:16], T.tr[:, :], Op.subtract)
-        tt(["P%d" % bank] + keys, ["nq"], T.nq[:, :], PS[bank][:, 0:16], xf[:, 0:16], Op.not_equal)
-        a()
-        tt(["td", "nq"], ["td"], T.td[:, :], T.td[:, :], T.nq[:, :], Op.mult)
-        b()
-        tt(["td", "tr"], ["td"], T.td[:, :], T.td[:, :], T.tr[:, :], Op.add)
-        c()
-        copy("v", ["td"], [of], T[of][:, :], T.td[:, :])
-
-    ts(["xi"], ["xk"], T.xk[:, :], T.xi[:, 16:48], 192, None, Op.bitwise_and)
-    ts(["xi"], ["xq"], T.xq[:, :], T.xi[:, 16:48], 1792, None, Op.bitwise_and)
-    copy("v", ["xi"], ["xu"], T.xu[:, :], T.xi[:, :])
-    copy("v", ["xi"], ["xf1"], T.xf1[:, 0:16], T.xi[:, 0:16])
-    fill("xf1e", T.xf1[:, 16:24], -1.0)
     ts(["jm"], ["n15"], T.n15[:, :], T.jm[:, :], 15.0, None, Op.is_lt)
     ts(["jm"], ["q15"], T.q15[:, :], T.jm[:, :], 15.0, None, Op.is_equal)
+    fill("wsel0", T.wsel[:, :], 0.0)
+
+    own1 = T.land1[:, 16 + 64 * me:16 + 64 * me + 64]
+
+    def columns(q, key, out, a, n):
+        copy(q, ["fb", "fc", "lt%d" % (a // 16)], [key], out, T.fbc[:, :].indirect(T["lt"][:, a:a + n]))
+
+    columns("v", "sb1a", T.sb1[:, 0:128], 0, 8)
+    columns("s", "sb1b", T.sb1[:, 128:256], 8, 8)
+    send("arr1", "sent1", turn[0:4], ["sb1a", "sb1b"], lambda i, r: T.sb1[:, 64 * i:64 * i + 64], own1)
+    columns("s", "sb1c", T.sb1[:, 256:448], 16, 12)
+    send("arr1", "sent1", turn[4:7], ["sb1c"], lambda i, r: T.sb1[:, 256 + 64 * i:320 + 64 * i], own1)
+    columns("s", "own1", own1, 28, 4)
+    for k in range(8):
+        dma("y", "da", ["sent1"], "fa", T.far[16 * k:16 * k + 16, :], T.fa[:, :])
+    for k in range(4):
+        dma("y", "df", [], "fa2", T.fa2[32 * k:32 * k + 32, :], T.fa[:, 512 * k:512 * k + 512])
+    iota("xf1e", T.xf1[:, 16:24], [[0, 8]], -1)
     op("g", ["n15"], ["sh1"], lambda e: e.affine_select(T.sh1[:, :], T.n15[:, :], [[-1, 128]], Op.is_equal, 0.0, -1, 1))
     op("g", ["q15"], ["sh15"], lambda e: e.affine_select(T.sh15[:, :], T.q15[:, :], [[-1, 128]], Op.is_equal, 0.0, 15, 1))
-    copy("v", IOT + ["xu"], ["xaf"], T.xaf[:, :], T.iot[:, :].indirect(T.xu[:, 0:16]))
-    ts(["em", "pf"], ["e8"], T.e8[:, :], T.em[:, :], T.pf[0:8, 0:1], None, Op.is_equal)
-    ts(["xk"], ["e1"], T.e1[:, :], T.xk[:, :], 7.0, None, Op.mult)
-    ts(["xq"], ["e2"], T.e2[:, :], T.xq[:, :], -0.75, None, Op.mult)
-    ts(["trb", "pq45"], ["tr"], T.tr[:, :], T.trb[:, :], T.pq[:, 4:5], None, Op.add)
-    fill("s1e", T.same1[:, 0:1], 0.0)
-    mm(["e8", "v8"], ["P1"], PS[1][:, 0:256], T.e8[:, :], T.v8[:, :])
-    shifted(T.xf1, ["xf1", "xf1e"], 2)
-    copy("s", ["P1"], ["vf"], T.vf[:, :], PS[1][:, 0:256])
-    tt(["e1", "xi"], ["e1"], T.e1[:, :], T.e1[:, :], T.xi[:, 16:48], Op.add)
-    tt(["xaf"], ["same1"], T.same1[:, 1:256], T.xaf[:, 1:256], T.xaf[:, 0:255], Op.is_equal)
-    tt(["e1", "e2"], ["e1"], T.e1[:, :], T.e1[:, :], T.e2[:, :], Op.add)
-    ends(T.xf1, ["xf1", "xf1e"], "of1", 2, (
-        lambda: copy("v", ["e1"], ["obc"], T.obc[:, :], T.e1[:, :]),
-        lambda: copy("v", ["a16"], ["a16b"], T.a16[:, 128:256], T.a16[:, 0:128]),
-        lambda: ts(["iot0", "pf"], ["ident"], T.ident[:, :], T.iot[:, 0:128], pf, None, Op.is_equal)))
+    iota("iot", T.iot[:, :], [[1, 2048]], 0)
 
-    L1 = ["in1", "own1"]
+    def fields(key, src, skey, k, q, e1, e2, m1, s1, m2, s2):
+        return [lambda: ts([skey], [key + "k"], k, src, m1, None, Op.bitwise_and),
+                lambda: ts([skey], [key + "q"], q, src, m2, None, Op.bitwise_and),
+                lambda: ts([key + "k"], [key + "1"], e1, k, s1, None, Op.mult),
+                lambda: ts([key + "q"], [key + "2"], e2, q, s2, None, Op.mult),
+                lambda: tt([key + "1", skey], [key + "1"], e1, e1, src, Op.add)]
 
-    def spread(k, bank, a, b):
-        mm(L1 + [SEL[k]], ["P%d" % bank], PS[bank][:, 0:b - a], T.selb[:, 128 * k:128 * k + 128], T.land1[:, a:b])
+    def shifted(xf, keys, bank):
+        mm(keys + ["sh1"], bank, PS[bank][:, 0:16], T.sh1[:, :], xf(0), True, False)
+        mm(keys + ["sh15"], bank, PS[bank][:, 0:16], T.sh15[:, :], xf(1), False, True)
 
-    for k in (4, 5, 6, 7, 0, 1):
-        spread(k, k, 0, 512)
-    spread(3, 3, 0, 256)
-    spread(2, 2, 0, 512)
-    for k in (4, 5, 6, 7):
-        copy("vs"[k % 2], ["P%d" % k], ["wc%d" % k], T.wc[:, 512 * k - 2048:512 * k - 1536], PS[k][:, :])
-    spread(3, 4, 256, 512)
+    def ends(xf, keys, n, bank):
+        eq, nu, of = "eq%d" % n, "nu%d" % n, "of%d" % n
+        return [lambda: tt(["P%d" % bank] + keys, [eq], T[eq][:, :], PS[bank][:, 0:16], xf(0), Op.is_equal),
+                lambda: tt(keys + ["tr"], ["td"], T.td[:, :], T.tr[:, :], xf(0), Op.subtract),
+                lambda: copy("v", [eq], [nu], T[nu][:, :], T[eq][:, :]),
+                lambda: tt(["td", eq], ["td"], T.td[:, :], T.td[:, :], T[eq][:, :], Op.mult),
+                lambda: tt(["td"] + keys, ["td"], T.td[:, :], T.td[:, :], xf(0), Op.add),
+                lambda: copy("v", ["td"], [of], T[of][:, :], T.td[:, :])]
 
-    def window_b(q, k, lo, n, bank):
-        copy(q, ["P%d" % bank], ["wb%d" % k], T.wb[:, lo:lo + n], PS[bank][:, 0:n])
+    def same(q, n):
+        at = 272 * (n - 1)
+        copy(q, ["nu%d" % n, "idx"], ["same%d" % n], T.same[:, at + 1:at + 257], T.idx[:, 0:16].indirect(T["nu%d" % n][:, :]))
 
-    window_b("s", 1, 512, 512, 1)
-    window_b("v", 0, 0, 512, 0)
-    tt(["wc4", "wc5", "wc6", "wc7", "obc", "vf"], ["w"], T.w[:, :], T.wc[:, :].indirect(T.obc[:, 16:32]), T.vf[:, :], Op.mult)
-    window_b("s", 2, 1024, 512, 2)
-    window_b("v", 3, 1536, 256, 3)
-    window_b("s", 4, 1792, 256, 4)
-    WB = ["wb%d" % k for k in range(5)]
-    tt(WB + ["obc", "w"], ["p1"], T.p1[:, :], T.wb[:, :].indirect(T.obc[:, 0:16]), T.w[:, :], Op.mult)
-    copy("s", IOT + ["xu"], ["xbf"], T.xbf[:, :], T.iot[:, :].indirect(T.xu[:, 16:32]))
-    copy("s", ["xaf", "xu"], ["xa2"], T.xa2[:, :], T.xaf[:, :].indirect(T.xu[:, 48:64]))
-    copy("s", ["xbf", "xu"], ["xb2"], T.xb2[:, :], T.xbf[:, :].indirect(T.xu[:, 48:64]))
-    zero("win2")
+    xs = fields("x", T.xi[:, 0:48], "xi", T.xk[:, :], T.xq[:, :], T.e1[:, :], T.e2[:, :], 96, 15.0, 1920, -0.75)
+    lp = fields("f", T.lai[:, :], "lai", T.lk[:, :], T.lq[:, :], T.f1[:, :], T.f2[:, :], 480, 3.0, 1536, -0.9375)
+    xs[0]()
+    xs[1]()
+    xs[2]()
+    xs[3]()
+    xs[4]()
+    copy("v", ["xi"], ["xf1"], T.xf1[:, 0:16], T.xi[:, 0:16])
+    tt(["x1", "x2"], ["xh"], T.xh[:, :], T.e1[:, 16:48], T.e2[:, 16:48], Op.add)
+    ts(["pm4"], ["bl1"], col(3), T.pm[:, 4:5], -32.0, 16.0, Op.mult, Op.add)
+    ts(["em"], ["e8"], T.e8[:, :], T.em[:, :], 0.0, None, Op.is_equal)
+    X1 = lambda s: T.xf1[:, s:s + 16]
+    W1.append(zero("win1", 1536, 2048))
+    W2 = [zero("win2", 0, 1024)]
+    CUTS = ((0, CUT1), (CUT1, 16))
+    for pair in range(4):
+        for f in range(2):
+            for a, b in CUTS:
+                for r in (2 * pair, 2 * pair + 1):
+                    at = 128 * f + 8 * a + (b - a) * r
+                    to_groups(["xh"], 2 + f, PS[2 + f][:, at:at + b - a], r,
+                              lambda rows: T.xh[rows, 16 * (1 - f) + a:16 * (1 - f) + b])
+    for f in range(2):
+        half = slice(64 * f, 64 * f + 64)
+        op("s", ["P%d" % (2 + f), "bl1"], ["cu1%d" % f], lambda e: e.activation(
+            T.cu1[half, :], PS[2 + f][half, 128 * f:128 * f + 128], RELU, bias=T.pq[half, 3:4]))
+    shifted(X1, ["xf1", "xf1e"], 4)
+    mm(["e8", "v8"], 5, PS[5][:, 0:256], T.e8[:, :], T.v8[:, :], rows=slice(0, 8))
+    e1 = ends(X1, ["xf1", "xf1e"], 1, 4)
+    in_turns(lp, [
+        lambda: ts(["trb", "p15"], ["tr"], T.tr[:, :], T.trb[:, :], col(1), None, Op.add),
+        lambda: ts(["jm", "p15", "wsel0"], ["wsel"], T.wsel[:, 112:128], T.jm[:, 0:16], col(1), None, Op.is_equal),
+        lambda: tt(["x1", "x2"], ["xa"], T.e1[:, 0:16], T.e1[:, 0:16], T.e2[:, 0:16], Op.add),
+        lambda: copy("v", ["xi"], ["xu1"], T.xu[:, 16:48], T.xi[:, 32:64]),
+        lambda: copy("v", ["xa"], ["xu0"], T.xu[:, 0:16], T.e1[:, 0:16])])
+    e1[1]()
+    ts(["cu10", "cu11"], ["l1"], T.l1[:, :], T.cu1[:, :], 528.0, None, Op.min)
+    in_turns([e1[0], e1[2], e1[3], e1[4], e1[5]], [
+        lambda: fill("se", T.same[:, 0::272], 0.0),
+        lambda: same("s", 1),
+        lambda: ts(["jm", "p15"], ["a16"], T.a16[:, :], T.jm[:, 0:16], col(1), None, Op.is_equal),
+        lambda: tt(["f1", "f2"], ["lpf"], T.f1[:, :], T.f1[:, :], T.f2[:, :], Op.add)])
+    copy("s", ["P5"], ["vf"], T.vf[:, :], PS[5][:, 0:256])
 
-    def slab_sums(p, pk, c, same, keys, win, of):
-        op("v", [pk] + keys, [c], lambda e: e.tensor_tensor_scan(T[c][:, :], same[:, :], p, 0.0, Op.mult, Op.add))
-        copy("v", [c, of], [win], T[win][:, :].indirect(T[of][:, :]), T[c][:, :])
+    L1 = ["arr1", "own1", "l1a", "l1b", "l1"]
+
+    def gather1(q, part, r0, r1):
+        a, b = CUTS[part]
+        lo, n = 8 * a + (b - a) * r0, (b - a) * (r1 - r0)
+        copy(q, L1, ["gb1%d%d" % (part, r) for r in range(r0, r1)], T.gb1[:, 16 * lo:16 * (lo + n)],
+             T.land1[:, :].indirect(T.l1[:, lo:lo + n]))
+
+    def select1(part):
+        a, b = CUTS[part]
+        for r in range(8):
+            lo = 16 * (8 * a + (b - a) * r)
+            for f in (1, 0):
+                rows = slice(64 * f, 64 * f + 64)
+                mm(["gb1%d%d" % (part, r), "wsel"], 2 * part + f, PS[2 * part + f][:, 0:16 * (b - a)],
+                   T.wsel[rows, 112 - 16 * r:240 - 16 * r], T.gb1[rows, lo:lo + 16 * (b - a)], r == 0, r == 7, rows)
+
+    def run_sums(n, part, a, b):
+        c, p, at = T["c%d" % n], T["p%d" % n], 272 * (n - 1)
+        first = [] if a == 0 else ["c%d%d" % (n, part - 1)]
+        op("v", ["p%d%d" % (n, part), "same%d" % n, "se"] + first, ["c%d%d" % (n, part)],
+           lambda e: e.tensor_tensor_scan(c[:, a:b], T.same[:, at + a:at + b], p[:, a:b], c[:, a - 1:a] if a else 0.0,
+                                          Op.mult, Op.add))
+
+    def products1(part):
+        a, b = (16 * x for x in CUTS[part])
+        return [lambda: tt(["P%d" % (2 * part + 1), "vf"], ["w%d" % part], T.w[:, a:b], PS[2 * part + 1][:, 0:b - a],
+                           T.vf[:, a:b], Op.mult),
+                lambda: tt(["P%d" % (2 * part), "w%d" % part], ["p1%d" % part], T.p1[:, a:b], PS[2 * part][:, 0:b - a],
+                           T.w[:, a:b], Op.mult),
+                lambda: run_sums(1, part, a, b)]
+
+    for q, r0, r1 in (("v", 0, 1), ("s", 1, 2), ("v", 2, 4), ("s", 4, 6), ("v", 6, 7), ("s", 7, 8)):
+        gather1(q, 0, r0, r1)
+    select1(0)
+    for q, r0, r1 in (("v", 0, 2), ("s", 2, 4), ("s", 4, 6), ("s", 6, 8)):
+        gather1(q, 1, r0, r1)
+    select1(1)
+    in_turns(products1(0), [lambda: ts(["p31"], ["ph"], col(4), col(0), 16.0, None, Op.is_ge),
+                            lambda: copy("v", ["lpf"], ["lph"], T.lph[:, :], T.f1[:, 0:16])])
+    in_turns(products1(1))
 
     def add_groups(bank, out, data, keys):
-        mm(keys + ["a16"], ["P%d" % bank], out, data, T.a16[:, 0:16])
+        mm(keys + ["a16"], bank, out, data, T.a16[:, :])
 
-    def block(i, b):
-        return i // 4, PS[i // 4][:, 32 * (i % 4) + b:32 * (i % 4) + 32:2]
+    def exchange(x, data, keys, out, between):
+        sb, land = T["sb%d" % x], T["land%d" % x]
+        for c, dests in enumerate(CALLS + [[me]]):
+            for i, r in enumerate(dests):
+                for b in range(2):
+                    add_groups(c, PS[c][:, 32 * i + b:32 * i + 32:2], data(r, b), keys(r, b))
+            a, n = 32 * dests[0], 32 * len(dests)
+            if c == len(CALLS):
+                out(["P%d" % c], ["own%d" % x], land[:, a:a + n], PS[c][:, 0:n], a, n)
+            else:
+                out(["P%d" % c], ["sb%d%d" % (x, c)], sb[:, a:a + n], PS[c][:, 0:n], a, n)
+                send("arr3%d" % c if x == 3 else "arr%d" % x, "sent", dests, ["sb%d%d" % (x, c)],
+                     lambda i, r: sb[:, 32 * r:32 * r + 32], land[:, 32 * me:32 * me + 32])
+            between[c]()
 
-    def to_owners(x, win, sb, land, between):
-        for i, q in enumerate(turn):
-            for b in range(2):
-                bank, out = block(i, b)
-                add_groups(bank, out, T[win][:, 256 * q + 128 * b:256 * q + 128 * b + 128], [win])
-        for h in range(2):
-            between[h]()
-            copy("v", ["P%d" % h], [sb + "ab"[h]], T[sb][:, 128 * h:128 * h + 128], PS[h][:, 0:128])
-            send(x, h, 32, [sb + "ab"[h]], T[sb], land)
+    def to_owners(x, n, parts, win, zeros, between):
+        copy("v", ["c%d%d" % (n, k) for k in range(parts)] + ["of%d" % n] + zeros, [win],
+             T[win][:, :].indirect(T["of%d" % n][:, :]), T["c%d" % n][:, :])
+        between[0]()
+        exchange(x, lambda r, b: T[win][:, 256 * r + 128 * b:256 * r + 128 * b + 128], lambda r, b: [win],
+                 lambda reads, writes, dst, src, a, m: copy("v", reads, writes, dst, src), between[1:])
 
-    def turn_back(x, land, r, at=0):
+    def by_column(x, win, zeros, lo):
+        land, r = T["land%d" % x], T["r%d" % x]
         for b in range(2):
-            transpose(["in%d" % x, "own%d" % x], ["P%d" % (2 + b)], PS[2 + b][:, 0:128], land[:, b::2])
-            copy("vs"[b], ["P%d" % (2 + b)], [r + "ab"[b]], T[r][:, at + 128 * b:at + 128 * b + 128], PS[2 + b][:, 0:128])
+            transpose(["arr%d" % x, "own%d" % x], 5 + b, PS[5 + b][:, 0:128], land[:, b::2])
+            copy("vs"[b], ["P%d" % (5 + b)], ["r%d%d" % (x, b)], r[:, 128 * b:128 * b + 128], PS[5 + b][:, 0:128])
+        for b in range(2):
+            copy("v", ["r%d%d" % (x, b), "lp"] + zeros, [win],
+                 T[win][:, :].indirect(T.lp[:, lo + 8 * b:lo + 8 * b + 8]), r[:, 128 * b:128 * b + 128])
 
-    def own_columns(r, win, lo):
-        copy("v", [r + "a", r + "b", "lu", win], [win], T[win][:, 0:2048].indirect(T.lu[:, lo:lo + 16]), T[r][:, :])
+    def rows(win, bank, ms):
+        for C in ms:
+            for u in range(2):
+                m = 8 * u + C
+                add_groups(bank, PS[bank][:, 32 * C + u:32 * C + 32:2], T[win][:, 128 * m:128 * m + 128], [win])
 
-    def gather_all(win, keys, lists, lkey, gb, place):
-        for k in range(8):
-            copy("vs"[k % 2], keys + [lkey], ["%s%d" % (gb, k)], T[gb][:, 256 * k:256 * k + 256],
-                 win.indirect(lists[:, 16 * k:16 * k + 16]))
-            for b in range(2):
-                bank, out = place(k, b)
-                add_groups(bank, out, T[gb][:, 256 * k + 128 * b:256 * k + 128 * b + 128], ["%s%d" % (gb, k)])
+    W2.append(zero("win2", 1024, 2048))
+    copy("s", ["iot", "xu0", "xu1"], ["xx"], T.xx[:, :], T.iot[:, :].indirect(T.xu[:, 0:32]))
 
-    DIAG = (("b", "xb2", "xf2"), ("a", "xa2", "xd"))
+    def lists_a():
+        ts(["idx", "ph"], ["c256"], T.pq[:, 6:8], T.idx[:, 0:2], col(4), 256.0, Op.is_equal, Op.mult)
+        ts(["idx", "ph"], ["t2"], T.pq[:, 12:14], T.idx[:, 0:2], col(4), 0.5, Op.is_equal, Op.mult)
+        for h in range(2):
+            ts(["xi", "c256"], ["ob2%d" % h], T.ob2[:, h::2], T.xi[:, 48:64], col(6 + h), None, Op.add)
+        copy("s", ["xx", "ob20", "ob21"], ["ex"], T.ex[:, :], T.xx[:, :].indirect(T.ob2[:, :]))
 
-    def masked():
-        for c, src, out in DIAG:
-            tt([src, "a16", "a16b"], ["d%s0" % c], T["d%s0" % c][:, :], T[src][:, :], T.a16[:, :], Op.mult)
+    def lists_b():
+        copy("v", ["lai"], ["lau0"], T.lau0[:, :], T.lai[:, 0:16])
+        ts(["idx", "pf"], ["ident"], T.ident[:, :], T.idx[:, :], pf, None, Op.is_equal)
+        copy("s", ["fa", "lau0"], ["fag"], T.fag[:, :], T.far[:, :].indirect(T.lau0[:, :]))
 
-    slab_sums(T.p1[:, :], "p1", "c1", T.same1, ["same1", "s1e"], "win1", "of1")
-    to_owners(2, "win1", "sb2", T.land2, (
-        lambda: tt(["xb2"], ["same2"], T.same2[:, 1:256], T.xb2[:, 1:256], T.xb2[:, 0:255], Op.is_equal), masked))
-    for i, r in enumerate(turn):
-        to_groups(["lhb", "llb"], 4, 16 * i, 16, r, T.lhb[:, 32:48], T.llb[:, 32:48])
-    copy("v", ["li"], ["lu"], T.lu[:, :], T.li[:, :])
-    copy("s", ["w", "xu"], ["w2"], T.w2[:, :], T.w[:, :].indirect(T.xu[:, 48:64]))
-    for n in range(1, 5):
-        for c, src, out in DIAG:
-            s = T["d%s%d" % (c, n - 1)]
-            dst, key = (T["d%s%d" % (c, n)][:, :], "d%s%d" % (c, n)) if n < 4 else (T[out][:, 0:16], out)
-            tt(["d%s%d" % (c, n - 1)], [key], dst, s[:, 0::2], s[:, 1::2], Op.add)
-        if n == 1:
-            fill("xf2e", T.xf2[:, 16:24], -1.0)
-        elif n == 2:
-            copy("v", ["P4"], ["lau"], T.lau[:, :], PS[4][:, 0:128])
-        elif n == 3:
-            fill("s2e", T.same2[:, 0:1], 0.0)
-            fill("r3e", T.r3[:, 0:8], 0.0)
-    copy("s", ["fa", "lu"], ["fag"], T.fag[:, :], T.far[:, :].indirect(T.lu[:, 32:48]))
-    for b in range(2):
-        transpose(["w2"], ["P5"], PS[5][:, 128 * b:128 * b + 128], T.w2[:, 128 * b:128 * b + 128])
-    shifted(T.xf2, ["xf2", "xf2e"], 6)
-    copy("s", ["P5"], ["w2t"], T.w2t[:, :], PS[5][:, 0:256])
-    for b in range(2):
-        transpose(["fag"], ["P7"], PS[7][:, 128 * b:128 * b + 128], T.fag[:, 128 * b:128 * b + 128])
-    FAT = []
-    for b in range(2):
-        for a, n, i in ((me + 1, n_ranks - 1 - me, 0), (0, me + 1, n_ranks - 1 - me)):
-            if n:
-                FAT.append("fat%d%d" % (b, a))
-                copy("s", ["P7"], [FAT[-1]], T.fat[:, 32 * i + b:32 * (i + n):2],
-                     PS[7][:, 128 * b + 16 * a:128 * b + 16 * (a + n)])
-    ends(T.xf2, ["xf2", "xf2e"], "of2", 6, (
-        lambda: copy("v", ["xd"], ["ahb"], T.ahb[:, :], T.xd[:, :]),
-        lambda: tt(["xd", "ahb"], ["alb"], T.alb[:, :], T.xd[:, :], T.ahb[:, :], Op.subtract),
-        lambda: (fill("r3f", T.r3[:, 264:272], 0.0),
-                 ts(["pq45"], ["pq6"], T.pq[:, 6:7], T.pq[:, 5:6], 256.0, -8.0, Op.mult, Op.add))))
-    turn_back(2, T.land2, "r2")
+    def lists_c():
+        ts(["t2", "p15"], ["pick"], T.pick[:, 0:2], T.pq[:, 12:14], col(1), 32.0, Op.add, Op.mult)
+        copy("v", ["lpf"], ["lp"], T.lp[:, :], T.f1[:, :])
+
+    nothing = lambda: None
     for r in range(8):
-        to_groups(["ahb", "alb"], 4, 16 * r, 16, r, T.ahb[:, :], T.alb[:, :])
-    own_columns("r2", "win2", 32)
-    gather_all(T.win2[:, :], ["win2"], T.lau, "lau", "gb2", block)
-    for h in range(2):
-        tt(["P%d" % h] + FAT, ["sb3" + "ab"[h]], T.sb3[:, 128 * h:128 * h + 128], PS[h][:, 0:128],
-           T.fat[:, 128 * h:128 * h + 128], Op.mult)
-        send(3, h, 32, ["sb3" + "ab"[h]], T.sb3, T.land3)
-    zero("win3")
-    ts(["P4", "pq6"], ["cu"], T.cu[:, :], PS[4][:, 0:128], T.pq[:, 6:7], 7.0, Op.subtract, Op.max)
-    ts(["cu"], ["l3"], T.l3[:, :], T.cu[:, :], 264.0, None, Op.min)
-
-    def rows_part(win, bank, blocks):
-        for blk in blocks:
-            add_groups(bank, PS[bank][:, blk:256:16], T[win][:, 128 * blk:128 * blk + 128], [win])
-
-    rows_part("win2", 7, range(8))
-    turn_back(3, T.land3, "r3", 8)
-    gather_all(T.r3[:, :], ["r3a", "r3b", "r3e", "r3f"], T.l3, "l3", "gb3",
-               lambda k, b: (b, PS[b][:, 16 * k:16 * k + 16]))
+        to_groups(["lph"], 7, PS[7][:, 16 * r:16 * r + 16], r, lambda rows_: T.lph[rows_, :])
+    to_owners(2, 1, 2, "win1", W1, (lists_a, lists_b, lists_c, nothing, nothing, nothing))
+    iota("xf2e", T.xf2[:, 32:40], [[0, 8]], -1)
+    iota("j32", T.j32[:, :], [[0, 5], [1, 32]], 0)
+    iota("dpb", T.dpb[:, :], [[32, 2], [1, 2], [0, 2]], 0)
+    iota("r3a", T.r3[:, 0:8], [[0, 8]], 0)
+    iota("r3b", T.r3[:, 520:528], [[0, 8]], 0)
     for b in range(2):
-        tt(["P%d" % b, "w2t"], ["pt%d" % b], T.pt[:, 128 * b:128 * b + 128], PS[b][:, 0:128],
-           T.w2t[:, 128 * b:128 * b + 128], Op.mult)
+        transpose(["fag"], 0, PS[0][:, 128 * b:128 * b + 128], T.fag[:, 128 * b:128 * b + 128])
+    copy("s", ["w0", "w1", "xu1"], ["w2"], T.w2[:, :], T.w[:, :].indirect(T.xu[:, 32:48]))
+    blocks_turned(["ex"], ["xt"], T.xt[:, :], T.ex[:, :])
     for b in range(2):
-        transpose(["pt%d" % b], ["P4"], PS[4][:, 128 * b:128 * b + 128], T.pt[:, 128 * b:128 * b + 128])
-    slab_sums(PS[4][:, 0:256], "P4", "c2", T.same2, ["same2", "s2e"], "win3", "of2")
-    to_owners(4, "win3", "sb4", T.land4, (lambda: zero("win4"), lambda: None))
-    rows_part("win2", 7, range(8, 16))
-    for h in range(2):
-        copy("v", ["P7"], ["ta%d" % h], T.ta[:, 128 * h:128 * h + 128], PS[7][:, 128 * h:128 * h + 128])
-        transpose(["ta%d" % h], ["P%d" % (5 + h)], PS[5 + h][:, 0:128], T.ta[:, 128 * h:128 * h + 128])
-    for h in range(2):
-        tt(["P%d" % (5 + h), "fa2"], ["ya%d" % h], T["ya%d" % h][:, :], PS[5 + h][:, 0:128],
-           T.fa2[:, 128 * h:128 * h + 128], Op.mult)
-        dma("y", "do", ["ya%d" % h], None, T.ya[8 * h:8 * h + 8, :], T["ya%d" % h][:, :])
-    turn_back(4, T.land4, "r4")
-    own_columns("r4", "win4", 0)
-    rows_part("win4", 4, range(16))
-    for h in range(2):
-        copy("v", ["P4"], ["tb%d" % h], T.tb[:, 128 * h:128 * h + 128], PS[4][:, 128 * h:128 * h + 128])
-        transpose(["tb%d" % h], ["P%d" % (5 + h)], PS[5 + h][:, 0:128], T.tb[:, 128 * h:128 * h + 128])
-    for h in range(2):
-        copy("sv"[h], ["P%d" % (5 + h)], ["yb%d" % h], T["yb%d" % h][:, :], PS[5 + h][:, 0:128])
-        dma("sy"[h], "do", ["yb%d" % h], None, T.yb[8 * h:8 * h + 8, :], T["yb%d" % h][:, :])
+        copy("s", ["P0"], ["fat%d" % b], T.fat[:, b::2], PS[0][:, 128 * b:128 * b + 128])
+    copy("v", ["P7"], ["lau"], T.lau[:, :], PS[7][:, 0:128])
+    copy("v", ["xt", "pick"], ["xf2"], T.xf2[:, 0:32], T.xt[:, :].indirect(T.pick[:, 0:2]))
+    X2 = lambda s: T.xf2[:, 16 + s:32 + s]
+    ts(["j32", "p31"], ["z32"], T.z32[:, :], T.j32[:, 16:144], col(0), None, Op.is_equal)
+    copy("v", ["xf2"], ["xah"], T.xah[:, :], T.xf2[:, 0:16])
+
+    by_column(2, "win2", W2, 0)
+    W3 = [zero("win3", 0, 768)]
+    for P in range(4):
+        for h in range(2):
+            mm(["xah", "z32"], 7, PS[7][:, 2 * P + h:64:8], T.z32[32 * P:32 * P + 32, :], T.xah[32 * P:32 * P + 32, h::2],
+               rows=slice(32 * P, 32 * P + 32))
+    shifted(X2, ["xf2", "xf2e"], 5)
+    e2 = ends(X2, ["xf2", "xf2e"], 2, 5)
+
+    def gather2(q, r, a, b):
+        copy(q, ["win2", "lau"], ["gb2%d%d" % (r, k) for k in range(a, b)], T.gb2[:, 256 * r + 128 * a:256 * r + 128 * b],
+             T.win2[:, :].indirect(T.lau[:, 16 * r + 8 * a:16 * r + 8 * b]))
+
+    order = [r for dests in CALLS for r in dests] + [me]
+    gather2("v", order[0], 0, 1)
+    gather2("s", order[0], 1, 2)
+    for k in range(1, 5):
+        gather2("sv"[k % 2], order[k], 0, 2)
+
+    def rest2():
+        gather2("v", order[5], 0, 2)
+        gather2("s", order[6], 0, 2)
+        gather2("s", order[7], 0, 2)
+
+    exchange(3, lambda r, b: T.gb2[:, 256 * r + 128 * b:256 * r + 128 * b + 128], lambda r, b: ["gb2%d%d" % (r, b)],
+             lambda reads, writes, dst, src, a, m: tt(reads + ["fat0", "fat1"], writes, dst, src, T.fat[:, a:a + m], Op.mult),
+             (rest2,
+              lambda: (ts(["dpb", "p15"], ["dpo"], T.dpo[:, :], T.dpb[:, :], col(1), col(1), Op.add, Op.add),
+                       ts(["p31", "pf"], ["bl3"], col(9), col(0), pf, 16.0, Op.subtract, Op.mult)),
+              lambda: ts(["P7", "bl3"], ["cu3"], T.cu3[:, :], PS[7][:, 0:64], col(9), -8.0, Op.add, Op.max),
+              e2[0],
+              lambda: ts(["cu3"], ["l3"], T.l3[:, :], T.cu3[:, :], 512.0, 8.0, Op.min, Op.add)))
+    rows("win2", 7, range(8))
+    e2[2]()
+    ts(["j32", "p31"], ["a32"], T.a32[:, :], T.j32[:, 0:32], col(0), None, Op.is_equal)
+    W3.append(zero("win3", 768, 1408))
+
+    R3 = ["r3a", "r3b", "l3"]
+    for key, dests in [("arr30", CALLS[0]), ("arr31", CALLS[1]), ("own3", [me]), ("arr32", CALLS[2]), ("arr33", CALLS[3])]:
+        a, n = dests[0], len(dests)
+        copy("s", [key, "dpo"], ["dup" + key], T.dup3[:, 64 * a:64 * (a + n)],
+             T.land3[:, 32 * a:32 * (a + n)].indirect(T.dpo[:, 0:4 * n]))
+        blocks_turned(["dup" + key], ["r3" + key], T.r3[:, 8 + 64 * a:8 + 64 * (a + n)], T.dup3[:, 64 * a:64 * (a + n)])
+        R3.append("r3" + key)
+        if key == "arr30":
+            blocks_turned(["w2"], ["w2t"], T.w2t[:, :], T.w2[:, :])
+
+    def gather3(q, a, b):
+        copy(q, R3, ["gb3%d" % C for C in range(a, b)], T.gb3[:, 128 * a:128 * b], T.r3[:, :].indirect(T.l3[:, 8 * a:8 * b]))
+
+    for q, a, b in (("v", 0, 1), ("s", 1, 2), ("v", 2, 3), ("s", 3, 4), ("v", 4, 6), ("s", 6, 8)):
+        gather3(q, a, b)
+    same("s", 2)
+    for part, (a, b) in enumerate(PARTS3):
+        for C in range(a, b):
+            mm(["gb3%d" % C, "a32"], part, PS[part][:, 32 * (C - a):32 * (C - a) + 32], T.gb3[:, 128 * C:128 * C + 128], T.a32[:, :])
+    W3.append(zero("win3", 1408, 2048))
+
+    def products2(part):
+        a, b = (32 * x for x in PARTS3[part])
+        return [lambda: tt(["P%d" % part, "w2t"], ["pt%d" % part], T.pt[:, a:b], PS[part][:, 0:b - a], T.w2t[:, a:b], Op.mult),
+                lambda: blocks_turned(["pt%d" % part], ["p2%d" % part], T.p2[:, a:b], T.pt[:, a:b]),
+                lambda: run_sums(2, part, a, b)]
+
+    in_turns(products2(0), [e2[1], e2[3], e2[4]])
+    in_turns(products2(1), [e2[5]])
+    W4 = [zero("win4", 0, 2048)]
+
+    def store(key, y, src):
+        for P in range(4):
+            dma("ys"[P % 2], "do", key, None, y[:, 512 * P:512 * P + 512], src[32 * P:32 * P + 32, :])
+
+    to_owners(4, 2, len(PARTS3), "win3", W3, (
+        lambda: blocks_turned(["P7"], ["ta"], T.ta[:, :], PS[7][:, 0:256]), nothing, nothing, nothing, nothing,
+        lambda: tt(["ta", "fa2"], ["yas"], T.yas[:, :], T.ta[:, :], T.fa2[:, :], Op.mult)))
+    store(["yas"], T.ya, T.yas)
+    by_column(4, "win4", W4, 16)
+    for k, (a, b) in enumerate(((0, 6), (6, 8))):
+        rows("win4", k, range(a, b))
+        blocks_turned(["P%d" % k], ["ybs%d" % k], T.ybs[:, 32 * a:32 * b], PS[k][:, 32 * a:32 * b])
+    store(["ybs0", "ybs1"], T.yb, T.ybs)
     for name in sorted(count):
         g.wait_ge(T.sem[name], count[name])

@@ -2,57 +2,56 @@ from concourse.bass import DstId, RemoteDMATransfer
 from concourse.mybir import AluOpType, ActivationFunctionType
 
 F32, BF, F16, I32, U16 = "float32", "bfloat16", "float16", "int32", "uint16"
-CUT1 = 10
+PARTS1 = ((0, 8), (8, 16))
 PARTS3 = ((0, 4), (4, 8))
 SCRATCH = {
     "pi": ("sbuf", [128, 8], I32), "pm": ("sbuf", [128, 8], I32), "pf": ("sbuf", [128, 8], F32),
     "pq": ("sbuf", [128, 16], F32), "ofu": ("sbuf", [128, 8], U16), "pick": ("sbuf", [128, 8], U16),
-    "jm": ("sbuf", [128, 128], BF), "idx": ("sbuf", [128, 128], BF), "j32": ("sbuf", [128, 160], BF),
-    "su": ("sbuf", [128, 256], F16), "z32": ("sbuf", [128, 128], F16), "wsel": ("sbuf", [128, 240], BF),
+    "jm": ("sbuf", [128, 128], BF), "idx": ("sbuf", [128, 256], BF), "j32": ("sbuf", [128, 160], BF),
+    "su": ("sbuf", [128, 256], F16), "z32": ("sbuf", [128, 144], F16),
+    "wsel": ("sbuf", [128, 224], BF), "swap": ("sbuf", [128, 256], BF),
     "a16": ("sbuf", [128, 16], F32), "a32": ("sbuf", [128, 32], F32),
     "em": ("sbuf", [8, 128], F32), "e8": ("sbuf", [8, 128], F32),
-    "iot": ("sbuf", [128, 2048], F32), "ident": ("sbuf", [128, 128], F32),
-    "q15": ("sbuf", [128, 128], F32), "n15": ("sbuf", [128, 128], F32),
-    "sh1": ("sbuf", [128, 128], F32), "sh15": ("sbuf", [128, 128], F32),
+    "iot": ("sbuf", [128, 2048], F32), "ident": ("sbuf", [128, 128], F32), "identb": ("sbuf", [128, 128], BF),
+    "pb": ("sbuf", [128, 128], BF), "sel8": ("sbuf", [128, 8], BF), "neg": ("sbuf", [128, 8], I32),
     "trb": ("sbuf", [128, 16], F32), "tr": ("sbuf", [128, 16], F32),
     "dpb": ("sbuf", [128, 8], F32), "dpo": ("sbuf", [128, 8], U16),
-    "li": ("sbuf", [128, 32], I32), "lai": ("sbuf", [128, 32], I32), "xi": ("sbuf", [128, 64], I32),
+    "li": ("sbuf", [128, 32], I32), "lai": ("sbuf", [128, 16], I32), "xi": ("sbuf", [128, 64], I32),
     "v8": ("sbuf", [8, 256], F32),
     "fbc": ("sbuf", [128, 2048], BF), "far": ("sbuf", [128, 2048], BF), "fa2": ("sbuf", [128, 256], BF),
     "lh": ("sbuf", [128, 32], F16), "rep": ("sbuf", [128, 256], F32), "lt": ("sbuf", [128, 32], U16),
     "xk": ("sbuf", [128, 48], I32), "xq": ("sbuf", [128, 48], I32),
     "e1": ("sbuf", [128, 48], F32), "e2": ("sbuf", [128, 48], F32), "xh": ("sbuf", [128, 32], F16),
-    "cu1": ("sbuf", [128, 128], F32), "l1": ("sbuf", [128, 128], U16),
+    "cu1": ("sbuf", [128, 64], F32), "l1": ("sbuf", [128, 64], U16),
     "xu": ("sbuf", [128, 48], U16), "ob2": ("sbuf", [128, 32], U16),
-    "lk": ("sbuf", [128, 32], I32), "lq": ("sbuf", [128, 32], I32),
-    "f1": ("sbuf", [128, 32], F32), "f2": ("sbuf", [128, 32], F32),
-    "lau0": ("sbuf", [128, 16], U16), "lp": ("sbuf", [128, 32], U16), "lph": ("sbuf", [128, 16], F16),
+    "lau0": ("sbuf", [128, 16], U16), "lbu": ("sbuf", [128, 16], U16), "lah": ("sbuf", [128, 16], F16),
     "lau": ("sbuf", [128, 128], U16),
+    "inv2": ("sbuf", [128, 2304], BF), "inv4": ("sbuf", [128, 2048], BF), "invt": ("sbuf", [128, 128], BF),
+    "l2": ("sbuf", [128, 128], U16), "l4": ("sbuf", [128, 128], U16),
     "xx": ("sbuf", [128, 512], F32), "ex": ("sbuf", [128, 512], F32), "xt": ("sbuf", [128, 512], F32),
     "xah": ("sbuf", [128, 16], F16), "cu3": ("sbuf", [128, 64], F32), "l3": ("sbuf", [128, 64], U16),
     "same": ("sbuf", [128, 544], F32),
-    "xf1": ("sbuf", [128, 24], F32), "xf2": ("sbuf", [128, 40], F32),
+    "xf2": ("sbuf", [128, 32], I32), "nx1": ("sbuf", [128, 16], I32), "nx2": ("sbuf", [128, 16], I32),
     "of1": ("sbuf", [128, 16], U16), "of2": ("sbuf", [128, 16], U16),
     "eq1": ("sbuf", [128, 16], F32), "eq2": ("sbuf", [128, 16], F32),
     "nu1": ("sbuf", [128, 16], U16), "nu2": ("sbuf", [128, 16], U16), "td": ("sbuf", [128, 16], F32),
-    "vf": ("sbuf", [128, 256], F32), "sb1": ("sbuf", [128, 448], BF), "land1": ("sbuf", [128, 544], BF),
-    "gb1": ("sbuf", [128, 2048], BF),
+    "vf": ("sbuf", [128, 256], F32), "sb1": ("sbuf", [128, 448], BF), "land1": ("sbuf", [128, 1568], BF),
+    "gb1": ("sbuf", [128, 1024], BF),
     "w": ("sbuf", [128, 256], F32), "w2": ("sbuf", [128, 256], F32), "w2t": ("sbuf", [128, 256], F32),
     "p1": ("sbuf", [128, 256], F32), "c1": ("sbuf", [128, 256], F32),
-    "win1": ("sbuf", [128, 2304], F32), "win2": ("sbuf", [128, 2048], F32),
-    "win3": ("sbuf", [128, 2304], F32), "win4": ("sbuf", [128, 2048], F32),
+    "win1": ("sbuf", [128, 2304], F32), "win2": ("sbuf", [128, 2048], F32), "gb": ("sbuf", [128, 2048], F32),
     "sb2": ("sbuf", [128, 256], F32), "land2": ("sbuf", [128, 256], F32), "r2": ("sbuf", [128, 256], F32),
-    "fag": ("sbuf", [128, 256], F32), "fat": ("sbuf", [128, 256], F32), "gb2": ("sbuf", [128, 2048], F32),
+    "fag": ("sbuf", [128, 256], F32), "fat": ("sbuf", [128, 256], F32),
     "sb3": ("sbuf", [128, 256], F32), "land3": ("sbuf", [128, 256], F32), "dup3": ("sbuf", [128, 512], F32),
     "r3": ("sbuf", [128, 528], F32), "gb3": ("sbuf", [128, 1024], F32),
-    "pt": ("sbuf", [128, 256], F32), "p2": ("sbuf", [128, 256], F32), "c2": ("sbuf", [128, 256], F32),
-    "sb4": ("sbuf", [128, 256], F32), "land4": ("sbuf", [128, 256], F32), "r4": ("sbuf", [128, 256], F32),
+    "pt": ("sbuf", [128, 256], F32), "p2": ("sbuf", [128, 256], F32), "c2": ("sbuf", [128, 264], F32),
+    "sb4": ("sbuf", [128, 256], F32), "land4": ("sbuf", [128, 256], F32), "r4": ("sbuf", [128, 264], F32),
     "ta": ("sbuf", [128, 256], F32), "yas": ("sbuf", [128, 256], F32), "ybs": ("sbuf", [128, 256], F32),
 }
 for _b in range(8):
     SCRATCH["ps%d" % _b] = ("psum", [128, 512], F32)
-SEMAPHORES = ["qg", "qv", "qs", "qt", "dl", "db", "dc", "dx", "dv", "da", "df", "dm", "do",
-              "arr1", "arr2", "arr30", "arr31", "arr32", "arr33", "arr4", "sent1", "sent"]
+SEMAPHORES = ["qg", "qv", "qs", "qt", "dl", "db", "dc", "dx", "dv", "da", "df", "dm", "dn", "do",
+              "arr10", "arr11", "arr12", "arr2", "arr30", "arr31", "arr32", "arr33", "arr4", "sent1", "sent"]
 
 
 def rank_program(g, core, T, topo):
@@ -62,7 +61,7 @@ def rank_program(g, core, T, topo):
     cores = T.cores
     n_ranks = len(cores)
     Op = AluOpType
-    COPY, RELU = ActivationFunctionType.Copy, ActivationFunctionType.Relu
+    COPY, IDENT, RELU = ActivationFunctionType.Copy, ActivationFunctionType.Identity, ActivationFunctionType.Relu
     Q = {"g": g, "v": g.vector, "s": g.scalar, "t": g.tensor, "y": g.sync}
     count, known, snap, written, readers = {}, {q: {} for q in Q}, {}, {}, {}
     turn = [me ^ j for j in sorted(range(1, n_ranks), key=lambda j: (topo.mates(core, cores[me ^ j]), j))]
@@ -129,9 +128,6 @@ def rank_program(g, core, T, topo):
         else:
             op("s", reads, writes, lambda e: e.activation(out, in_, COPY))
 
-    def fill(key, out, c):
-        op("v", [], [key], lambda e: e.memset(out, c))
-
     tile = {}
 
     def tensor(reads, bank, rows, fn):
@@ -152,10 +148,11 @@ def rank_program(g, core, T, topo):
 
     def iota(key, out, pattern, base, per_row=0):
         op("g", [], [key], lambda e: e.iota(out, pattern, base, per_row, allow_small_or_imprecise_dtypes=True))
+        return key
 
-    def zero(win, a, b, reads=("fb", "fc"), src=None):
+    def fill(win, a, b, reads=("fb", "fc"), src=None, value=0.0):
         key = "%s@%d" % (win, a)
-        op("s", list(reads), [key], lambda e: e.activation(T[win][:, a:b], src or T.fbc[:, a:b], COPY, scale=0.0))
+        op("s", list(reads), [key], lambda e: e.activation(T[win][:, a:b], src or T.fbc[:, a:b], IDENT, bias=value, scale=0.0))
         return key
 
     def send(arr, sent, dests, reads, src, land):
@@ -164,7 +161,7 @@ def rank_program(g, core, T, topo):
         for i, r in enumerate(dests):
             rid, pid = topo.addr(cores[r], core)
             eng = topo.engines(core, cores[r])
-            n = 1 << ((len(eng) // len(dests)).bit_length() - 1)
+            n = len(eng) // len(dests)
             trs.append(RemoteDMATransfer(
                 dst_ids=[DstId(rid=rid, pnc=pid)], dma_engine_mask=sum(1 << e for e in eng[n * i:n * i + n]),
                 remote_sem=T.sem[arr], srcs=[src(i, r)], dsts=[land], alu_op=0))
@@ -180,7 +177,17 @@ def rank_program(g, core, T, topo):
                 if k < len(c):
                     c[k]()
 
+    def nothing():
+        pass
+
     PS = [T["ps%d" % b] for b in range(8)]
+
+    def next_table(n, src, reads):
+        nx, key = T["nx%d" % n], "nx%d" % n
+        for k in range(8):
+            dma("y", "dn", reads, None, nx[16 * k:16 * k + 15, :], src(slice(16 * k + 1, 16 * k + 16), 0, 16))
+        dma("y", "dn", [], None, nx[15::16, 0:15], src(slice(0, 128, 16), 1, 16))
+        dma("y", "dn", ["neg"], key, nx[15::16, 15:16], T.neg[0:8, 0:1])
 
     dma("y", "dl", [], "li", T.li[:, 0:16], T.lb[:, :])
     dma("s", "dl", [], "li", T.li[:, 16:32], T.lc[:, :])
@@ -190,21 +197,22 @@ def rank_program(g, core, T, topo):
     for k, x in enumerate((T.xa, T.xc, T.xb, T.ob)):
         dma("y", "dx", [], "xi", T.xi[:, 16 * k:16 * k + 16], x[:, :])
     dma("y", "dv", [], "v8", T.v8[:, :], T.v[:, :])
-    dma("y", "dm", [], "lai", T.lai[:, 0:16], T.la[:, :])
-    dma("y", "dm", [], "lai", T.lai[:, 16:32], T.lb[:, :])
+    dma("y", "dm", [], "lai", T.lai[:, :], T.la[:, :])
 
     op("g", [], ["pi"], lambda e: e.iota(T.pi[:, 0:1], [[0, 1]], 0, 1))
     iota("jm", T.jm[:, :], [[0, 8], [1, 16]], 0)
     iota("pf", T.pf[:, 0:1], [[0, 1]], 0, 1)
-    iota("l1a", T.land1[:, 0:16], [[0, 16]], 0)
-    iota("l1b", T.land1[:, 528:544], [[0, 16]], 0)
-    iota("idx", T.idx[:, :], [[1, 128]], 0)
-    iota("em", T.em[:, :], [[1, 8], [0, 16]], 0, -1)
+    op("g", [], ["neg"], lambda e: e.iota(T.neg[:, 0:1], [[0, 1]], -1, 0))
     iota("trb", T.trb[:, :], [[16, 16]], 2048)
+    iota("l1a", T.land1[:, 0:16], [[0, 16]], 0)
+    iota("l1b", T.land1[:, 1552:1568], [[0, 16]], 0)
+    iota("idx", T.idx[:, :], [[1, 256]], 0)
+    iota("j32", T.j32[:, :], [[0, 5], [1, 32]], 0)
+    next_table(1, lambda rows, a, b: T.xa[rows, a:b], [])
     pf = T.pf[:, 0:1]
-    W1 = [zero("win1", 0, 128, ["jm"], T.jm[:, :])]
-    for a, b in ((128, 256), (256, 512), (512, 1024), (1024, 1536)):
-        W1.append(zero("win1", a, b, list(W1), T.win1[:, 0:b - a]))
+    W1 = [fill("win1", a, a + 128, ["jm"], T.jm[:, :]) for a in (0, 128)]
+    for a in (256, 512):
+        W1.append(fill("win1", a, a + 256, W1[0:2], T.win1[:, 0:256]))
 
     def bits(j, m):
         ts(["pi"], ["pm%d" % j], T.pm[:, j:j + 1], T.pi[:, 0:1], m, None, Op.bitwise_and)
@@ -217,139 +225,135 @@ def rank_program(g, core, T, topo):
 
     bits(0, 31)
     bits(2, 2)
+    bits(4, 48)
     copy("v", ["pm0"], ["p31"], col(0), T.pm[:, 0:1])
     bits(3, 12)
+    bits(5, 64)
     ts(["jm", "p31"], ["su0"], T.su[:, 0:128], T.jm[:, :], col(0), None, Op.is_equal)
-    bits(4, 48)
     ts(["jm", "p31"], ["su1"], T.su[:, 128:256], T.jm[:, :], 16.0, col(0), Op.add, Op.is_equal)
     more(2, 3.0, "pf", col(2), "o1", pf)
-    bits(5, 64)
-    more(3, 7.0, "o1", col(10), "o2", col(2))
-    bits(1, 15)
-    more(4, -0.875, "o2", col(2), "o3", col(10))
+    ts(["pm4"], ["o2"], col(10), T.pm[:, 4:5], -0.875, None, Op.mult)
 
     def to_groups(reads, bank, out, r, table):
         rows = slice(32 * (r // 2), 32 * (r // 2) + 32)
-        mm(reads + ["su%d" % (r % 2)], bank, out, T.su[rows, 128 * (r % 2):128 * (r % 2) + 128], table(rows), rows=rows)
+        mm(reads + ["su%d" % (r % 2)], bank, out, T.su[rows, 128 * (r % 2):128 * (r % 2) + 128], table[rows, :], rows=rows)
 
     copy("v", ["li"], ["lh"], T.lh[:, :], T.li[:, :])
-    more(5, -0.75, "o3", T.ofu[:, 0:1], "ofu", col(2))
-    copy("v", ["pm1"], ["p15"], col(1), T.pm[:, 1:2])
-    for i, r in enumerate(turn + [me]):
-        to_groups(["lh"], i // 4, PS[i // 4][:, 32 * (i % 4):32 * (i % 4) + 32], r, lambda rows: T.lh[rows, :])
+    more(3, 7.0, "o1", col(11), "o3", col(2))
+    more(5, -0.75, "o2", col(14), "o4", col(10))
+    side = n_ranks // 2
+    turn1 = [r for r in turn if r // side != me // side] + [r for r in turn if r // side == me // side]
+    for i, r in enumerate(turn1 + [me]):
+        to_groups(["lh"], i // 2, PS[i // 2][:, 32 * (i % 2):32 * (i % 2) + 32], r, T.lh)
+    bits(1, 15)
+    ts(["o3", "o4"], ["ofu"], T.ofu[:, 0:1], col(11), col(14), None, Op.add)
+    for k in range(4):
+        copy("vs"[k % 2], ["P%d" % k], ["rep%d" % k], T.rep[:, 64 * k:64 * k + 64], PS[k][:, 0:64])
     for h in range(2):
-        copy("v", ["P%d" % h], ["rep%d" % h], T.rep[:, 128 * h:128 * h + 128], PS[h][:, 0:128])
-    for h in range(2):
-        copy("v", ["rep%d" % h, "ofu"], ["lt%d" % h], T["lt"][:, 16 * h:16 * h + 16],
+        copy("v", ["rep%d" % (2 * h), "rep%d" % (2 * h + 1), "ofu"], ["lt%d" % h], T["lt"][:, 16 * h:16 * h + 16],
              T.rep[:, 128 * h:128 * h + 128].indirect(T.ofu[:, 0:1]))
-    ts(["jm"], ["n15"], T.n15[:, :], T.jm[:, :], 15.0, None, Op.is_lt)
-    ts(["jm"], ["q15"], T.q15[:, :], T.jm[:, :], 15.0, None, Op.is_equal)
-    fill("wsel0", T.wsel[:, :], 0.0)
+    W1.append(fill("win1", 768, 1024, W1[0:2], T.win1[:, 0:256]))
+    copy("v", ["pm1"], ["p15"], col(1), T.pm[:, 1:2])
+    ts(["p31"], ["ph"], col(4), col(0), 16.0, None, Op.is_ge)
 
-    own1 = T.land1[:, 16 + 64 * me:16 + 64 * me + 64]
+    own1 = T.land1[:, 528 + 64 * me:528 + 64 * me + 64]
 
     def columns(q, key, out, a, n):
         copy(q, ["fb", "fc", "lt%d" % (a // 16)], [key], out, T.fbc[:, :].indirect(T["lt"][:, a:a + n]))
 
     columns("v", "sb1a", T.sb1[:, 0:128], 0, 8)
     columns("s", "sb1b", T.sb1[:, 128:256], 8, 8)
-    send("arr1", "sent1", turn[0:4], ["sb1a", "sb1b"], lambda i, r: T.sb1[:, 64 * i:64 * i + 64], own1)
+    send("arr10", "sent1", turn1[0:4], ["sb1a", "sb1b"], lambda i, r: T.sb1[:, 64 * i:64 * i + 64], own1)
     columns("s", "sb1c", T.sb1[:, 256:448], 16, 12)
-    send("arr1", "sent1", turn[4:7], ["sb1c"], lambda i, r: T.sb1[:, 256 + 64 * i:320 + 64 * i], own1)
+    send("arr11", "sent1", turn1[4:6], ["sb1c"], lambda i, r: T.sb1[:, 256 + 64 * i:320 + 64 * i], own1)
+    send("arr12", "sent1", turn1[6:7], ["sb1c"], lambda i, r: T.sb1[:, 384:448], own1)
     columns("s", "own1", own1, 28, 4)
     for k in range(8):
         dma("y", "da", ["sent1"], "fa", T.far[16 * k:16 * k + 16, :], T.fa[:, :])
-    for k in range(4):
-        dma("y", "df", [], "fa2", T.fa2[32 * k:32 * k + 32, :], T.fa[:, 512 * k:512 * k + 512])
-    iota("xf1e", T.xf1[:, 16:24], [[0, 8]], -1)
-    op("g", ["n15"], ["sh1"], lambda e: e.affine_select(T.sh1[:, :], T.n15[:, :], [[-1, 128]], Op.is_equal, 0.0, -1, 1))
-    op("g", ["q15"], ["sh15"], lambda e: e.affine_select(T.sh15[:, :], T.q15[:, :], [[-1, 128]], Op.is_equal, 0.0, 15, 1))
+    for h in range(2):
+        dma("y", "df", [], "fa2", T.fa2[:, 128 * h:128 * h + 128], T.fa[8 * h:8 * h + 8, :])
+    iota("em", T.em[:, :], [[1, 8], [0, 16]], 0, -1)
     iota("iot", T.iot[:, :], [[1, 2048]], 0)
 
-    def fields(key, src, skey, k, q, e1, e2, m1, s1, m2, s2):
-        return [lambda: ts([skey], [key + "k"], k, src, m1, None, Op.bitwise_and),
-                lambda: ts([skey], [key + "q"], q, src, m2, None, Op.bitwise_and),
-                lambda: ts([key + "k"], [key + "1"], e1, k, s1, None, Op.mult),
-                lambda: ts([key + "q"], [key + "2"], e2, q, s2, None, Op.mult),
-                lambda: tt([key + "1", skey], [key + "1"], e1, e1, src, Op.add)]
-
-    def shifted(xf, keys, bank):
-        mm(keys + ["sh1"], bank, PS[bank][:, 0:16], T.sh1[:, :], xf(0), True, False)
-        mm(keys + ["sh15"], bank, PS[bank][:, 0:16], T.sh15[:, :], xf(1), False, True)
-
-    def ends(xf, keys, n, bank):
+    def ends(x, key, n):
         eq, nu, of = "eq%d" % n, "nu%d" % n, "of%d" % n
-        return [lambda: tt(["P%d" % bank] + keys, [eq], T[eq][:, :], PS[bank][:, 0:16], xf(0), Op.is_equal),
-                lambda: tt(keys + ["tr"], ["td"], T.td[:, :], T.tr[:, :], xf(0), Op.subtract),
+        return [lambda: tt(["nx%d" % n, key], [eq], T[eq][:, :], T["nx%d" % n][:, :], x, Op.is_equal),
                 lambda: copy("v", [eq], [nu], T[nu][:, :], T[eq][:, :]),
-                lambda: tt(["td", eq], ["td"], T.td[:, :], T.td[:, :], T[eq][:, :], Op.mult),
-                lambda: tt(["td"] + keys, ["td"], T.td[:, :], T.td[:, :], xf(0), Op.add),
+                lambda: tt(["tr", eq], ["td"], T.td[:, :], T.tr[:, :], T[eq][:, :], Op.mult),
+                lambda: tt(["td", key], ["td"], T.td[:, :], T.td[:, :], x, Op.max),
                 lambda: copy("v", ["td"], [of], T[of][:, :], T.td[:, :])]
 
     def same(q, n):
         at = 272 * (n - 1)
         copy(q, ["nu%d" % n, "idx"], ["same%d" % n], T.same[:, at + 1:at + 257], T.idx[:, 0:16].indirect(T["nu%d" % n][:, :]))
 
-    xs = fields("x", T.xi[:, 0:48], "xi", T.xk[:, :], T.xq[:, :], T.e1[:, :], T.e2[:, :], 96, 15.0, 1920, -0.75)
-    lp = fields("f", T.lai[:, :], "lai", T.lk[:, :], T.lq[:, :], T.f1[:, :], T.f2[:, :], 480, 3.0, 1536, -0.9375)
-    xs[0]()
-    xs[1]()
-    xs[2]()
-    xs[3]()
-    xs[4]()
-    copy("v", ["xi"], ["xf1"], T.xf1[:, 0:16], T.xi[:, 0:16])
+    x3 = T.xi[:, 0:48]
+    e1 = ends(T.xi[:, 0:16], "xi", 1)
+    ts(["xi"], ["xk"], T.xk[:, :], x3, 96, None, Op.bitwise_and)
+    ts(["xi"], ["xq"], T.xq[:, :], x3, 1920, None, Op.bitwise_and)
+    ts(["j32", "p31"], ["z32"], T.z32[:, :], T.j32[:, 0:144], col(0), None, Op.is_equal)
+    ts(["xk"], ["x1"], T.e1[:, :], T.xk[:, :], 15.0, None, Op.mult)
+    ts(["xq"], ["x2"], T.e2[:, :], T.xq[:, :], -0.75, None, Op.mult)
+    ts(["pm4"], ["bl1"], col(3), T.pm[:, 4:5], -32.0, 528.0, Op.mult, Op.add)
+    tt(["x1", "xi"], ["x1"], T.e1[:, :], T.e1[:, :], x3, Op.add)
+    e1[0]()
     tt(["x1", "x2"], ["xh"], T.xh[:, :], T.e1[:, 16:48], T.e2[:, 16:48], Op.add)
-    ts(["pm4"], ["bl1"], col(3), T.pm[:, 4:5], -32.0, 16.0, Op.mult, Op.add)
-    ts(["em"], ["e8"], T.e8[:, :], T.em[:, :], 0.0, None, Op.is_equal)
-    X1 = lambda s: T.xf1[:, s:s + 16]
-    W1.append(zero("win1", 1536, 2048))
-    W2 = [zero("win2", 0, 1024)]
-    CUTS = ((0, CUT1), (CUT1, 16))
+    op("s", ["trb", "p15"], ["tr"], lambda e: e.activation(T.tr[:, :], T.trb[:, :], IDENT, bias=col(1)))
+    wsel0 = fill("wsel", 0, 224)
+    op("s", ["fb"], ["se"], lambda e: e.activation(T.same[:, 0::272], T.fbc[:, 0:2], COPY, scale=0.0))
+    W1.append(fill("win1", 1024, 2048))
     for pair in range(4):
+        rows = slice(32 * pair, 32 * pair + 32)
         for f in range(2):
-            for a, b in CUTS:
-                for r in (2 * pair, 2 * pair + 1):
-                    at = 128 * f + 8 * a + (b - a) * r
-                    to_groups(["xh"], 2 + f, PS[2 + f][:, at:at + b - a], r,
-                              lambda rows: T.xh[rows, 16 * (1 - f) + a:16 * (1 - f) + b])
+            for a, b in PARTS1:
+                at = 4 * a + (b - a) * pair
+                mm(["xh", "z32"], 4 + f, PS[4 + f][:, at:at + b - a], T.z32[rows, 0:128],
+                   T.xh[rows, 16 * (1 - f) + a:16 * (1 - f) + b], rows=rows)
+    in_turns(e1[1:], [
+        lambda: ts(["ph", "pf"], ["to"], col(8), col(4), 96.0, pf, Op.mult, Op.add),
+        lambda: ts(["idx", "p31", wsel0], ["wsel"], T.wsel[:, 96:128], T.idx[:, 0:32], col(0), None, Op.is_equal),
+        lambda: ts(["idx", "to"], ["swap"], T.swap[:, :], T.idx[:, :], -16.0, col(8), Op.add, Op.is_equal),
+        lambda: ts(["em"], ["e8"], T.e8[:, :], T.em[:, :], 0.0, None, Op.is_equal)])
+    mm(["e8", "v8"], 6, PS[6][:, 0:256], T.e8[:, :], T.v8[:, :], rows=slice(0, 8))
     for f in range(2):
         half = slice(64 * f, 64 * f + 64)
-        op("s", ["P%d" % (2 + f), "bl1"], ["cu1%d" % f], lambda e: e.activation(
-            T.cu1[half, :], PS[2 + f][half, 128 * f:128 * f + 128], RELU, bias=T.pq[half, 3:4]))
-    shifted(X1, ["xf1", "xf1e"], 4)
-    mm(["e8", "v8"], 5, PS[5][:, 0:256], T.e8[:, :], T.v8[:, :], rows=slice(0, 8))
-    e1 = ends(X1, ["xf1", "xf1e"], 1, 4)
-    in_turns(lp, [
-        lambda: ts(["trb", "p15"], ["tr"], T.tr[:, :], T.trb[:, :], col(1), None, Op.add),
-        lambda: ts(["jm", "p15", "wsel0"], ["wsel"], T.wsel[:, 112:128], T.jm[:, 0:16], col(1), None, Op.is_equal),
-        lambda: tt(["x1", "x2"], ["xa"], T.e1[:, 0:16], T.e1[:, 0:16], T.e2[:, 0:16], Op.add),
-        lambda: copy("v", ["xi"], ["xu1"], T.xu[:, 16:48], T.xi[:, 32:64]),
-        lambda: copy("v", ["xa"], ["xu0"], T.xu[:, 0:16], T.e1[:, 0:16])])
-    e1[1]()
-    ts(["cu10", "cu11"], ["l1"], T.l1[:, :], T.cu1[:, :], 528.0, None, Op.min)
-    in_turns([e1[0], e1[2], e1[3], e1[4], e1[5]], [
-        lambda: fill("se", T.same[:, 0::272], 0.0),
-        lambda: same("s", 1),
-        lambda: ts(["jm", "p15"], ["a16"], T.a16[:, :], T.jm[:, 0:16], col(1), None, Op.is_equal),
-        lambda: tt(["f1", "f2"], ["lpf"], T.f1[:, :], T.f1[:, :], T.f2[:, :], Op.add)])
-    copy("s", ["P5"], ["vf"], T.vf[:, :], PS[5][:, 0:256])
+        op("s", ["P%d" % (4 + f), "bl1"], ["cu1%d" % f], lambda e: e.activation(
+            T.cu1[half, :], PS[4 + f][half, 0:64], RELU, bias=T.pq[half, 3:4]))
+    same("s", 1)
+    tt(["x1", "x2"], ["xa"], T.e1[:, 0:16], T.e1[:, 0:16], T.e2[:, 0:16], Op.add)
+    ts(["cu10", "cu11"], ["l1"], T.l1[:, :], T.cu1[:, :], 1552.0, None, Op.min)
+    ts(["jm", "p15"], ["a16"], T.a16[:, :], T.jm[:, 0:16], col(1), None, Op.is_equal)
+    copy("v", ["xa"], ["xu0"], T.xu[:, 0:16], T.e1[:, 0:16])
+    copy("v", ["xi"], ["xu1"], T.xu[:, 16:48], T.xi[:, 32:64])
+    ts(["idx", "ph"], ["c256"], T.pq[:, 6:8], T.idx[:, 0:2], col(4), 256.0, Op.is_equal, Op.mult)
+    copy("s", ["P6"], ["vf"], T.vf[:, :], PS[6][:, 0:256])
+    copy("v", ["lai"], ["lah"], T.lah[:, :], T.lai[:, :])
+    for h in range(2):
+        ts(["xi", "c256"], ["ob2%d" % h], T.ob2[:, h::2], T.xi[:, 48:64], col(6 + h), None, Op.add)
 
-    L1 = ["arr1", "own1", "l1a", "l1b", "l1"]
+    L1 = ["l1a", "l1b", "l1"]
+    for c, (keys, ranks) in enumerate(((["arr10"], turn1[0:4]), (["arr11"], turn1[4:6]), (["arr12", "own1"], [turn1[6], me]))):
+        a, n = 64 * min(ranks), 64 * len(ranks)
+        for u in range(2):
+            bank = 2 * c + u
+            mm(keys + ["swap"], bank, PS[bank][:, 0:n], T.swap[:, 128 * u:128 * u + 128], T.land1[:, 528 + a:528 + a + n])
+            L1.append("side%d%d" % (c, u))
+            copy("vs"[u], ["P%d" % bank], [L1[-1]], T.land1[:, 16 + 1024 * u + a:16 + 1024 * u + a + n], PS[bank][:, 0:n])
 
     def gather1(q, part, r0, r1):
-        a, b = CUTS[part]
-        lo, n = 8 * a + (b - a) * r0, (b - a) * (r1 - r0)
+        a, b = PARTS1[part]
+        lo, n = 4 * a + (b - a) * r0, (b - a) * (r1 - r0)
         copy(q, L1, ["gb1%d%d" % (part, r) for r in range(r0, r1)], T.gb1[:, 16 * lo:16 * (lo + n)],
              T.land1[:, :].indirect(T.l1[:, lo:lo + n]))
 
     def select1(part):
-        a, b = CUTS[part]
-        for r in range(8):
-            lo = 16 * (8 * a + (b - a) * r)
+        a, b = PARTS1[part]
+        for r in range(4):
+            lo = 16 * (4 * a + (b - a) * r)
             for f in (1, 0):
                 rows = slice(64 * f, 64 * f + 64)
                 mm(["gb1%d%d" % (part, r), "wsel"], 2 * part + f, PS[2 * part + f][:, 0:16 * (b - a)],
-                   T.wsel[rows, 112 - 16 * r:240 - 16 * r], T.gb1[rows, lo:lo + 16 * (b - a)], r == 0, r == 7, rows)
+                   T.wsel[rows, 96 - 32 * r:224 - 32 * r], T.gb1[rows, lo:lo + 16 * (b - a)], r == 0, r == 3, rows)
 
     def run_sums(n, part, a, b):
         c, p, at = T["c%d" % n], T["p%d" % n], 272 * (n - 1)
@@ -359,22 +363,22 @@ def rank_program(g, core, T, topo):
                                           Op.mult, Op.add))
 
     def products1(part):
-        a, b = (16 * x for x in CUTS[part])
+        a, b = (16 * x for x in PARTS1[part])
         return [lambda: tt(["P%d" % (2 * part + 1), "vf"], ["w%d" % part], T.w[:, a:b], PS[2 * part + 1][:, 0:b - a],
                            T.vf[:, a:b], Op.mult),
                 lambda: tt(["P%d" % (2 * part), "w%d" % part], ["p1%d" % part], T.p1[:, a:b], PS[2 * part][:, 0:b - a],
                            T.w[:, a:b], Op.mult),
                 lambda: run_sums(1, part, a, b)]
 
-    for q, r0, r1 in (("v", 0, 1), ("s", 1, 2), ("v", 2, 4), ("s", 4, 6), ("v", 6, 7), ("s", 7, 8)):
-        gather1(q, 0, r0, r1)
+    for r in range(4):
+        gather1("vs"[r % 2], 0, r, r + 1)
     select1(0)
-    for q, r0, r1 in (("v", 0, 2), ("s", 2, 4), ("s", 4, 6), ("s", 6, 8)):
+    for q, r0, r1 in (("v", 0, 1), ("s", 1, 3), ("s", 3, 4)):
         gather1(q, 1, r0, r1)
     select1(1)
-    in_turns(products1(0), [lambda: ts(["p31"], ["ph"], col(4), col(0), 16.0, None, Op.is_ge),
-                            lambda: copy("v", ["lpf"], ["lph"], T.lph[:, :], T.f1[:, 0:16])])
-    in_turns(products1(1))
+    p, q = products1(0), products1(1)
+    for step in (p[0], p[1], q[0], p[2], q[1], q[2]):
+        step()
 
     def add_groups(bank, out, data, keys):
         mm(keys + ["a16"], bank, out, data, T.a16[:, :])
@@ -384,7 +388,7 @@ def rank_program(g, core, T, topo):
         for c, dests in enumerate(CALLS + [[me]]):
             for i, r in enumerate(dests):
                 for b in range(2):
-                    add_groups(c, PS[c][:, 32 * i + b:32 * i + 32:2], data(r, b), keys(r, b))
+                    add_groups(c, PS[c][:, 32 * i + b:32 * i + 32:2], data[:, 256 * r + 128 * b:256 * r + 128 * b + 128], keys(r, b))
             a, n = 32 * dests[0], 32 * len(dests)
             if c == len(CALLS):
                 out(["P%d" % c], ["own%d" % x], land[:, a:a + n], PS[c][:, 0:n], a, n)
@@ -394,104 +398,118 @@ def rank_program(g, core, T, topo):
                      lambda i, r: sb[:, 32 * r:32 * r + 32], land[:, 32 * me:32 * me + 32])
             between[c]()
 
-    def to_owners(x, n, parts, win, zeros, between):
-        copy("v", ["c%d%d" % (n, k) for k in range(parts)] + ["of%d" % n] + zeros, [win],
-             T[win][:, :].indirect(T["of%d" % n][:, :]), T["c%d" % n][:, :])
-        between[0]()
-        exchange(x, lambda r, b: T[win][:, 256 * r + 128 * b:256 * r + 128 * b + 128], lambda r, b: [win],
-                 lambda reads, writes, dst, src, a, m: copy("v", reads, writes, dst, src), between[1:])
+    def as_it_is(reads, writes, dst, src, a, n):
+        copy("v", reads, writes, dst, src)
 
-    def by_column(x, win, zeros, lo):
+    def gathers(win, keys, table, order):
+        def piece(q, r, a, b):
+            copy(q, keys, ["gb%d%d" % (r, k) for k in range(a, b)], T.gb[:, 256 * r + 128 * a:256 * r + 128 * b],
+                 win.indirect(table[:, 16 * r + 8 * a:16 * r + 8 * b]))
+        for k in range(2):
+            piece("v", order[k], 0, 1)
+            piece("s", order[k], 1, 2)
+        for k in range(2, 5):
+            piece("vss"[k - 2], order[k], 0, 2)
+        return lambda: [piece("vss"[k - 5], order[k], 0, 2) for k in range(5, 8)]
+
+    ORDER = [r for dests in CALLS for r in dests] + [me]
+
+    def gathered(r, b):
+        return ["gb%d%d" % (r, b)]
+
+    def turn_back(x):
         land, r = T["land%d" % x], T["r%d" % x]
         for b in range(2):
             transpose(["arr%d" % x, "own%d" % x], 5 + b, PS[5 + b][:, 0:128], land[:, b::2])
             copy("vs"[b], ["P%d" % (5 + b)], ["r%d%d" % (x, b)], r[:, 128 * b:128 * b + 128], PS[5 + b][:, 0:128])
-        for b in range(2):
-            copy("v", ["r%d%d" % (x, b), "lp"] + zeros, [win],
-                 T[win][:, :].indirect(T.lp[:, lo + 8 * b:lo + 8 * b + 8]), r[:, 128 * b:128 * b + 128])
 
-    def rows(win, bank, ms):
-        for C in ms:
-            for u in range(2):
-                m = 8 * u + C
-                add_groups(bank, PS[bank][:, 32 * C + u:32 * C + 32:2], T[win][:, 128 * m:128 * m + 128], [win])
+    def inverse(n, lst, none, bank, turner):
+        inv = T["inv%d" % n]
+        return [lambda a=0, b=2: copy("v", [lst, "idx"] + none, ["inv%d" % n], inv[:, :].indirect(T[lst][:, 8 * a:8 * b]),
+                                      T.idx[:, 128 * a:128 * b]),
+                lambda: [mm(["inv%d" % n, "sel8"], bank, PS[bank][:, a:128:16], inv[:, a:2048:16], T.sel8[:, :]) for a in range(16)],
+                lambda q: copy(q, ["P%d" % bank], ["invt"], T.invt[:, :], PS[bank][:, 0:128]),
+                lambda: mm(["invt", turner], bank, PS[bank][:, 128:256], T.invt[:, :], T[turner][:, :]),
+                lambda: copy("v", ["P%d" % bank], ["l%d" % n], T["l%d" % n][:, :], PS[bank][:, 128:256])]
 
-    W2.append(zero("win2", 1024, 2048))
+    W2 = [fill("win2", 0, 512)]
     copy("s", ["iot", "xu0", "xu1"], ["xx"], T.xx[:, :], T.iot[:, :].indirect(T.xu[:, 0:32]))
-
-    def lists_a():
-        ts(["idx", "ph"], ["c256"], T.pq[:, 6:8], T.idx[:, 0:2], col(4), 256.0, Op.is_equal, Op.mult)
-        ts(["idx", "ph"], ["t2"], T.pq[:, 12:14], T.idx[:, 0:2], col(4), 0.5, Op.is_equal, Op.mult)
-        for h in range(2):
-            ts(["xi", "c256"], ["ob2%d" % h], T.ob2[:, h::2], T.xi[:, 48:64], col(6 + h), None, Op.add)
-        copy("s", ["xx", "ob20", "ob21"], ["ex"], T.ex[:, :], T.xx[:, :].indirect(T.ob2[:, :]))
+    copy("s", ["xx", "ob20", "ob21"], ["ex"], T.ex[:, :], T.xx[:, :].indirect(T.ob2[:, :]))
 
     def lists_b():
-        copy("v", ["lai"], ["lau0"], T.lau0[:, :], T.lai[:, 0:16])
-        ts(["idx", "pf"], ["ident"], T.ident[:, :], T.idx[:, :], pf, None, Op.is_equal)
-        copy("s", ["fa", "lau0"], ["fag"], T.fag[:, :], T.far[:, :].indirect(T.lau0[:, :]))
+        ts(["t2", "p15"], ["pick"], T.pick[:, 0:2], T.pq[:, 12:14], col(1), 32.0, Op.add, Op.mult)
+        copy("v", ["P7"], ["lau"], T.lau[:, :], PS[7][:, 0:128])
 
     def lists_c():
-        ts(["t2", "p15"], ["pick"], T.pick[:, 0:2], T.pq[:, 12:14], col(1), 32.0, Op.add, Op.mult)
-        copy("v", ["lpf"], ["lp"], T.lp[:, :], T.f1[:, :])
+        copy("v", ["li"], ["lbu"], T.lbu[:, :], T.li[:, 0:16])
+        ts(["idx", "pf"], ["sel8"], T.sel8[:, :], T.idx[:, 0:128:16], pf, None, Op.is_equal)
 
-    nothing = lambda: None
+    def lists_d():
+        ts(["j32", "p31"], ["a32"], T.a32[:, :], T.j32[:, 0:32], col(0), None, Op.is_equal)
+        ts(["idx", "pf"], ["identb"], T.identb[:, :], T.idx[:, 0:128], pf, None, Op.is_equal)
+
+    def lists_e():
+        ts(["p31", "pf"], ["b16"], col(9), col(0), pf, 16.0, Op.subtract, Op.mult)
+
     for r in range(8):
-        to_groups(["lph"], 7, PS[7][:, 16 * r:16 * r + 16], r, lambda rows_: T.lph[rows_, :])
-    to_owners(2, 1, 2, "win1", W1, (lists_a, lists_b, lists_c, nothing, nothing, nothing))
-    iota("xf2e", T.xf2[:, 32:40], [[0, 8]], -1)
-    iota("j32", T.j32[:, :], [[0, 5], [1, 32]], 0)
+        to_groups(["lah"], 7, PS[7][:, 16 * r:16 * r + 16], r, T.lah)
+    copy("v", ["c10", "c11", "of1"] + W1, ["win1"], T.win1[:, :].indirect(T.of1[:, :]), T.c1[:, :])
+    copy("v", ["lai"], ["lau0"], T.lau0[:, :], T.lai[:, :])
+    ts(["idx", "ph"], ["t2"], T.pq[:, 12:14], T.idx[:, 0:2], col(4), 0.5, Op.is_equal, Op.mult)
+    ts(["idx", "pf"], ["ident"], T.ident[:, :], T.idx[:, 0:128], pf, None, Op.is_equal)
+    copy("s", ["fa", "lau0"], ["fag"], T.fag[:, :], T.far[:, :].indirect(T.lau0[:, :]))
+    W2.append(fill("win2", 512, 2048))
+    copy("s", ["w0", "w1", "xu1"], ["w2"], T.w2[:, :], T.w[:, :].indirect(T.xu[:, 32:48]))
+    exchange(2, T.win1, lambda r, b: ["win1"], as_it_is,
+             (lists_b, lists_c, lists_d, lists_e, lambda: blocks_turned(["ex"], ["xt"], T.xt[:, :], T.ex[:, :])))
     iota("dpb", T.dpb[:, :], [[32, 2], [1, 2], [0, 2]], 0)
     iota("r3a", T.r3[:, 0:8], [[0, 8]], 0)
     iota("r3b", T.r3[:, 520:528], [[0, 8]], 0)
+    iota("c2z", T.c2[:, 256:264], [[0, 8]], 0)
+    none2 = [iota("inv2@0", T.inv2[:, 0:768], [[0, 768]], 256)]
     for b in range(2):
         transpose(["fag"], 0, PS[0][:, 128 * b:128 * b + 128], T.fag[:, 128 * b:128 * b + 128])
-    copy("s", ["w0", "w1", "xu1"], ["w2"], T.w2[:, :], T.w[:, :].indirect(T.xu[:, 32:48]))
-    blocks_turned(["ex"], ["xt"], T.xt[:, :], T.ex[:, :])
+    ts(["b16"], ["bl3"], col(15), col(9), 8.0, None, Op.add)
+    copy("v", ["xt", "pick"], ["xf2"], T.xf2[:, :], T.xt[:, :].indirect(T.pick[:, 0:2]))
+    next_table(2, lambda rows, a, b: T.xf2[rows, 16 + a:16 + b], ["xf2"])
+    e2 = ends(T.xf2[:, 16:32], "xf2", 2)
     for b in range(2):
-        copy("s", ["P0"], ["fat%d" % b], T.fat[:, b::2], PS[0][:, 128 * b:128 * b + 128])
-    copy("v", ["P7"], ["lau"], T.lau[:, :], PS[7][:, 0:128])
-    copy("v", ["xt", "pick"], ["xf2"], T.xf2[:, 0:32], T.xt[:, :].indirect(T.pick[:, 0:2]))
-    X2 = lambda s: T.xf2[:, 16 + s:32 + s]
-    ts(["j32", "p31"], ["z32"], T.z32[:, :], T.j32[:, 16:144], col(0), None, Op.is_equal)
+        copy("sv"[b], ["P0"], ["fat%d" % b], T.fat[:, b::2], PS[0][:, 128 * b:128 * b + 128])
+    ts(["dpb", "p15"], ["dpo"], T.dpo[:, :], T.dpb[:, :], col(1), col(1), Op.add, Op.add)
+    none2.append(fill("inv2", 768, 1664, value=256.0))
     copy("v", ["xf2"], ["xah"], T.xah[:, :], T.xf2[:, 0:16])
+    blocks_turned(["w2"], ["w2t"], T.w2t[:, :], T.w2[:, :])
 
-    by_column(2, "win2", W2, 0)
-    W3 = [zero("win3", 0, 768)]
+    turn_back(2)
+    for b in range(2):
+        copy("v", ["r2%d" % b, "lau0"] + W2, ["win2"],
+             T.win2[:, :].indirect(T.lau0[:, 8 * b:8 * b + 8]), T.r2[:, 128 * b:128 * b + 128])
+    none2.append(fill("inv2", 1664, 2048, value=256.0))
     for P in range(4):
+        rows = slice(32 * P, 32 * P + 32)
         for h in range(2):
-            mm(["xah", "z32"], 7, PS[7][:, 2 * P + h:64:8], T.z32[32 * P:32 * P + 32, :], T.xah[32 * P:32 * P + 32, h::2],
-               rows=slice(32 * P, 32 * P + 32))
-    shifted(X2, ["xf2", "xf2e"], 5)
-    e2 = ends(X2, ["xf2", "xf2e"], 2, 5)
+            mm(["xah", "z32"], 7, PS[7][:, 2 * P + h:64:8], T.z32[rows, 16:144], T.xah[rows, h::2], rows=rows)
+    rest = gathers(T.win2[:, :], ["win2", "lau"], T.lau, ORDER)
+    ends2 = inverse(2, "of2", none2, 5, "identb")
 
-    def gather2(q, r, a, b):
-        copy(q, ["win2", "lau"], ["gb2%d%d" % (r, k) for k in range(a, b)], T.gb2[:, 256 * r + 128 * a:256 * r + 128 * b],
-             T.win2[:, :].indirect(T.lau[:, 16 * r + 8 * a:16 * r + 8 * b]))
-
-    order = [r for dests in CALLS for r in dests] + [me]
-    gather2("v", order[0], 0, 1)
-    gather2("s", order[0], 1, 2)
-    for k in range(1, 5):
-        gather2("sv"[k % 2], order[k], 0, 2)
-
-    def rest2():
-        gather2("v", order[5], 0, 2)
-        gather2("s", order[6], 0, 2)
-        gather2("s", order[7], 0, 2)
-
-    exchange(3, lambda r, b: T.gb2[:, 256 * r + 128 * b:256 * r + 128 * b + 128], lambda r, b: ["gb2%d%d" % (r, b)],
+    exchange(3, T.gb, gathered,
              lambda reads, writes, dst, src, a, m: tt(reads + ["fat0", "fat1"], writes, dst, src, T.fat[:, a:a + m], Op.mult),
-             (rest2,
-              lambda: (ts(["dpb", "p15"], ["dpo"], T.dpo[:, :], T.dpb[:, :], col(1), col(1), Op.add, Op.add),
-                       ts(["p31", "pf"], ["bl3"], col(9), col(0), pf, 16.0, Op.subtract, Op.mult)),
-              lambda: ts(["P7", "bl3"], ["cu3"], T.cu3[:, :], PS[7][:, 0:64], col(9), -8.0, Op.add, Op.max),
-              e2[0],
-              lambda: ts(["cu3"], ["l3"], T.l3[:, :], T.cu3[:, :], 512.0, 8.0, Op.min, Op.add)))
-    rows("win2", 7, range(8))
-    e2[2]()
-    ts(["j32", "p31"], ["a32"], T.a32[:, :], T.j32[:, 0:32], col(0), None, Op.is_equal)
-    W3.append(zero("win3", 768, 1408))
+             (lambda: (rest(), op("s", ["P7", "bl3"], ["cu3"],
+                                  lambda e: e.activation(T.cu3[:, :], PS[7][:, 0:64], RELU, bias=col(15)))),
+              lambda: (e2[0](), e2[2]()),
+              lambda: (e2[1](), e2[3](), same("s", 2)),
+              e2[4],
+              lambda: (ends2[0](), ts(["cu3"], ["l3"], T.l3[:, :], T.cu3[:, :], 520.0, None, Op.min))))
+    iota("r4z", T.r4[:, 256:264], [[0, 8]], 0)
+    iota("pb0", T.pb[:, :], [[2, 16], [32, 4], [1, 2]], 0)
+    none4 = [iota("inv4@0", T.inv4[:, :], [[0, 2048]], 256)]
+
+    def rows_a(blocks):
+        for blk in blocks:
+            add_groups(7, PS[7][:, blk:256:16], T.win2[:, 128 * blk:128 * blk + 128], ["win2"])
+
+    rows_a(range(8))
+    ends2[1]()
 
     R3 = ["r3a", "r3b", "l3"]
     for key, dests in [("arr30", CALLS[0]), ("arr31", CALLS[1]), ("own3", [me]), ("arr32", CALLS[2]), ("arr33", CALLS[3])]:
@@ -500,19 +518,18 @@ def rank_program(g, core, T, topo):
              T.land3[:, 32 * a:32 * (a + n)].indirect(T.dpo[:, 0:4 * n]))
         blocks_turned(["dup" + key], ["r3" + key], T.r3[:, 8 + 64 * a:8 + 64 * (a + n)], T.dup3[:, 64 * a:64 * (a + n)])
         R3.append("r3" + key)
-        if key == "arr30":
-            blocks_turned(["w2"], ["w2t"], T.w2t[:, :], T.w2[:, :])
+    ends2[2]("s")
+    ends2[3]()
 
     def gather3(q, a, b):
         copy(q, R3, ["gb3%d" % C for C in range(a, b)], T.gb3[:, 128 * a:128 * b], T.r3[:, :].indirect(T.l3[:, 8 * a:8 * b]))
 
     for q, a, b in (("v", 0, 1), ("s", 1, 2), ("v", 2, 3), ("s", 3, 4), ("v", 4, 6), ("s", 6, 8)):
         gather3(q, a, b)
-    same("s", 2)
     for part, (a, b) in enumerate(PARTS3):
         for C in range(a, b):
             mm(["gb3%d" % C, "a32"], part, PS[part][:, 32 * (C - a):32 * (C - a) + 32], T.gb3[:, 128 * C:128 * C + 128], T.a32[:, :])
-    W3.append(zero("win3", 1408, 2048))
+    rows_a(range(8, 16))
 
     def products2(part):
         a, b = (32 * x for x in PARTS3[part])
@@ -520,22 +537,37 @@ def rank_program(g, core, T, topo):
                 lambda: blocks_turned(["pt%d" % part], ["p2%d" % part], T.p2[:, a:b], T.pt[:, a:b]),
                 lambda: run_sums(2, part, a, b)]
 
-    in_turns(products2(0), [e2[1], e2[3], e2[4]])
-    in_turns(products2(1), [e2[5]])
-    W4 = [zero("win4", 0, 2048)]
+    p, q = products2(0), products2(1)
+    for step in (p[0], ends2[4], p[1], q[0], p[2], q[1], q[2]):
+        step()
 
-    def store(key, y, src):
-        for P in range(4):
-            dma("ys"[P % 2], "do", key, None, y[:, 512 * P:512 * P + 512], src[32 * P:32 * P + 32, :])
+    slots = inverse(4, "lbu", none4, 0, "pb")
+    rest = gathers(T.c2[:, :], ["c20", "c21", "c2z", "l2"], T.l2, ORDER)
+    exchange(4, T.gb, gathered, as_it_is, (
+        lambda: (rest(), copy("s", ["P7"], ["ta"], T.ta[:, :], PS[7][:, 0:256])),
+        lambda: slots[0](0, 1), nothing, lambda: slots[0](1, 2),
+        lambda: ts(["pb0", "pf"], ["pb"], T.pb[:, :], T.pb[:, :], pf, None, Op.is_equal)))
+    slots[1]()
+    slots[2]("s")
 
-    to_owners(4, 2, len(PARTS3), "win3", W3, (
-        lambda: blocks_turned(["P7"], ["ta"], T.ta[:, :], PS[7][:, 0:256]), nothing, nothing, nothing, nothing,
-        lambda: tt(["ta", "fa2"], ["yas"], T.yas[:, :], T.ta[:, :], T.fa2[:, :], Op.mult)))
-    store(["yas"], T.ya, T.yas)
-    by_column(4, "win4", W4, 16)
-    for k, (a, b) in enumerate(((0, 6), (6, 8))):
-        rows("win4", k, range(a, b))
-        blocks_turned(["P%d" % k], ["ybs%d" % k], T.ybs[:, 32 * a:32 * b], PS[k][:, 32 * a:32 * b])
-    store(["ybs0", "ybs1"], T.yb, T.ybs)
+    slots[3]()
+    slots[4]()
+    turn_back(4)
+    for h in range(2):
+        transpose(["ta"], 7, PS[7][:, 128 * h:128 * h + 128], T.ta[:, 128 * h:128 * h + 128])
+    for q, a, b in [("vs"[k % 2], k, k + 1) for k in range(4)] + [("vs"[k % 2], 2 * k, 2 * k + 2) for k in range(2, 8)]:
+        copy(q, ["r40", "r41", "r4z", "l4"], ["gb%d%d" % divmod(m, 2) for m in range(a, b)], T.gb[:, 128 * a:128 * b],
+             T.r4[:, :].indirect(T.l4[:, 8 * a:8 * b]))
+    tt(["P7", "fa2"], ["yas"], T.yas[:, :], PS[7][:, 0:256], T.fa2[:, :], Op.mult)
+    for h in range(2):
+        dma("y", "do", ["yas"], None, T.ya[8 * h:8 * h + 8, :], T.yas[:, 128 * h:128 * h + 128])
+    for m in range(16):
+        u, C = divmod(m, 8)
+        bank = 2 + C // 6
+        add_groups(bank, PS[bank][:, 32 * C + u:32 * C + 32:2], T.gb[:, 128 * m:128 * m + 128], gathered(*divmod(m, 2)))
+    for k, (a, b) in enumerate(((0, 192), (192, 256))):
+        blocks_turned(["P%d" % (2 + k)], ["ybs%d" % k], T.ybs[:, a:b], PS[2 + k][:, a:b])
+    for P in range(4):
+        dma("ys"[P % 2], "do", ["ybs0", "ybs1"], None, T.yb[:, 512 * P:512 * P + 512], T.ybs[32 * P:32 * P + 32, :])
     for name in sorted(count):
         g.wait_ge(T.sem[name], count[name])

from concourse.bass import DstId, RemoteDMATransfer
from concourse.mybir import AluOpType, ActivationFunctionType

F32, BF, F16, I32, U16 = "float32", "bfloat16", "float16", "int32", "uint16"
PARTS1 = ((0, 8), (8, 16))
PARTS3 = ((0, 4), (4, 8))
SCRATCH = {
    "pi": ("sbuf", [128, 8], I32), "pm": ("sbuf", [128, 8], I32), "pf": ("sbuf", [128, 8], F32),
    "pq": ("sbuf", [128, 16], F32), "ofu": ("sbuf", [128, 8], U16), "pick": ("sbuf", [128, 8], U16),
    "jm": ("sbuf", [128, 128], BF), "idx": ("sbuf", [128, 256], BF), "j32": ("sbuf", [128, 160], BF),
    "su": ("sbuf", [128, 256], F16), "z32": ("sbuf", [128, 144], F16),
    "wsel": ("sbuf", [128, 224], BF), "swap": ("sbuf", [128, 256], BF),
    "a16": ("sbuf", [128, 16], F32), "a32": ("sbuf", [128, 32], F32),
    "em": ("sbuf", [8, 128], F32), "e8": ("sbuf", [8, 128], F32),
    "iot": ("sbuf", [128, 2048], F32), "ident": ("sbuf", [128, 128], F32), "identb": ("sbuf", [128, 128], BF),
    "pb": ("sbuf", [128, 128], BF), "sel8": ("sbuf", [128, 8], BF), "neg": ("sbuf", [128, 8], I32),
    "trb": ("sbuf", [128, 16], F32), "tr": ("sbuf", [128, 16], F32),
    "dpb": ("sbuf", [128, 8], F32), "dpo": ("sbuf", [128, 8], U16),
    "li": ("sbuf", [128, 32], I32), "lai": ("sbuf", [128, 16], I32), "xi": ("sbuf", [128, 64], I32),
    "v8": ("sbuf", [8, 256], F32),
    "fbc": ("sbuf", [128, 2048], BF), "far": ("sbuf", [128, 2048], BF), "fa2": ("sbuf", [128, 256], BF),
    "lh": ("sbuf", [128, 32], F16), "rep": ("sbuf", [128, 256], F32), "lt": ("sbuf", [128, 32], U16),
    "xk": ("sbuf", [128, 48], I32), "xq": ("sbuf", [128, 48], I32),
    "e1": ("sbuf", [128, 48], F32), "e2": ("sbuf", [128, 48], F32), "xh": ("sbuf", [128, 32], F16),
    "cu1": ("sbuf", [128, 64], F32), "l1": ("sbuf", [128, 64], U16),
    "xu": ("sbuf", [128, 48], U16), "ob2": ("sbuf", [128, 32], U16),
    "lau0": ("sbuf", [128, 16], U16), "lbu": ("sbuf", [128, 16], U16), "lah": ("sbuf", [128, 16], F16),
    "lau": ("sbuf", [128, 128], U16),
    "inv2": ("sbuf", [128, 2304], BF), "inv4": ("sbuf", [128, 2048], BF), "invt": ("sbuf", [128, 128], BF),
    "l2": ("sbuf", [128, 128], U16), "l4": ("sbuf", [128, 128], U16),
    "xx": ("sbuf", [128, 512], F32), "ex": ("sbuf", [128, 512], F32), "xt": ("sbuf", [128, 512], F32),
    "xah": ("sbuf", [128, 16], F16), "cu3": ("sbuf", [128, 64], F32), "l3": ("sbuf", [128, 64], U16),
    "same": ("sbuf", [128, 544], F32),
    "xf2": ("sbuf", [128, 32], I32), "nx1": ("sbuf", [128, 16], I32), "nx2": ("sbuf", [128, 16], I32),
    "of1": ("sbuf", [128, 16], U16), "of2": ("sbuf", [128, 16], U16),
    "eq1": ("sbuf", [128, 16], F32), "eq2": ("sbuf", [128, 16], F32),
    "nu1": ("sbuf", [128, 16], U16), "nu2": ("sbuf", [128, 16], U16), "td": ("sbuf", [128, 16], F32),
    "vf": ("sbuf", [128, 256], F32), "sb1": ("sbuf", [128, 448], BF), "land1": ("sbuf", [128, 1568], BF),
    "gb1": ("sbuf", [128, 1024], BF),
    "w": ("sbuf", [128, 256], F32), "w2": ("sbuf", [128, 256], F32), "w2t": ("sbuf", [128, 256], F32),
    "p1": ("sbuf", [128, 256], F32), "c1": ("sbuf", [128, 256], F32),
    "win1": ("sbuf", [128, 2304], F32), "win2": ("sbuf", [128, 2048], F32), "gb": ("sbuf", [128, 2048], F32),
    "sb2": ("sbuf", [128, 256], F32), "land2": ("sbuf", [128, 256], F32), "r2": ("sbuf", [128, 256], F32),
    "fag": ("sbuf", [128, 256], F32), "fat": ("sbuf", [128, 256], F32),
    "sb3": ("sbuf", [128, 256], F32), "land3": ("sbuf", [128, 256], F32), "dup3": ("sbuf", [128, 512], F32),
    "r3": ("sbuf", [128, 528], F32), "gb3": ("sbuf", [128, 1024], F32),
    "pt": ("sbuf", [128, 256], F32), "p2": ("sbuf", [128, 256], F32), "c2": ("sbuf", [128, 264], F32),
    "sb4": ("sbuf", [128, 256], F32), "land4": ("sbuf", [128, 256], F32), "r4": ("sbuf", [128, 264], F32),
    "ta": ("sbuf", [128, 256], F32), "yas": ("sbuf", [128, 256], F32), "ybs": ("sbuf", [128, 256], F32),
}
for _b in range(8):
    SCRATCH["ps%d" % _b] = ("psum", [128, 512], F32)
SEMAPHORES = ["qg", "qv", "qs", "qt", "dl", "db", "dc", "dx", "dv", "da", "df", "dm", "dn", "do",
              "arr10", "arr11", "arr12", "arr2", "arr30", "arr31", "arr32", "arr33", "arr4", "sent1", "sent"]


def rank_program(g, core, T, topo):
    me = T.rank_of(core)
    if me is None:
        return
    cores = T.cores
    n_ranks = len(cores)
    Op = AluOpType
    COPY, IDENT, RELU = ActivationFunctionType.Copy, ActivationFunctionType.Identity, ActivationFunctionType.Relu
    Q = {"g": g, "v": g.vector, "s": g.scalar, "t": g.tensor, "y": g.sync}
    count, known, snap, written, readers = {}, {q: {} for q in Q}, {}, {}, {}
    turn = [me ^ j for j in sorted(range(1, n_ranks), key=lambda j: (topo.mates(core, cores[me ^ j]), j))]
    CALLS = [sorted(turn[a:a + 2]) for a in range(0, n_ranks - 1, 2)]

    def learn(q, tok):
        name, n = tok
        if known[q].get(name, 0) < n:
            known[q][name] = n
        for k, m in snap.get(tok, {}).items():
            if known[q].get(k, 0) < m:
                known[q][k] = m

    def need(q, toks):
        for tok in sorted(set(toks), key=lambda t: (-t[1], t[0])):
            if known[q].get(tok[0], 0) < tok[1]:
                Q[q].wait_ge(T.sem[tok[0]], tok[1])
                learn(q, tok)

    def before(q, reads, writes):
        toks = [written[k] for k in reads]
        for k in writes:
            if k in written and not (q == "t" and written[k][0] == "qt"):
                toks.append(written[k])
        for k in writes + [k for k in reads if k[0] == "P"]:
            toks += [t for t in readers.get(k, []) if t[0] != "q" + q]
        need(q, toks)

    def after(tok, reads, writes):
        for k in reads:
            readers.setdefault(k, []).append(tok)
        for k in writes:
            written[k] = tok
            readers[k] = []

    def op(q, reads, writes, fn):
        before(q, reads, writes)
        name = "q" + q
        count[name] = count.get(name, 0) + 1
        fn(Q[q]).then_inc(T.sem[name], 1)
        tok = (name, count[name])
        snap[tok] = dict(known[q])
        after(tok, reads, writes)

    def dma(q, sem, reads, key, out, in_):
        before(q, reads, [])
        Q[q].dma_start(out, in_).then_inc(T.sem[sem], 16)
        count[sem] = count.get(sem, 0) + 16
        if key:
            written[key] = (sem, count[sem])

    def tt(reads, writes, out, a, b, o):
        op("v", reads, writes, lambda e: e.tensor_tensor(out, a, b, o))

    def ts(reads, writes, out, a, s1, s2, o0, o1=None):
        if o1 is None:
            op("v", reads, writes, lambda e: e.tensor_scalar(out, a, s1, None, o0))
        else:
            op("v", reads, writes, lambda e: e.tensor_scalar(out, a, s1, s2, o0, o1))

    def copy(q, reads, writes, out, in_):
        if q == "v":
            op("v", reads, writes, lambda e: e.tensor_copy(out, in_))
        else:
            op("s", reads, writes, lambda e: e.activation(out, in_, COPY))

    tile = {}

    def tensor(reads, bank, rows, fn):
        key = "P%d" % bank
        if key in written and tile.get(key) != rows:
            need("t", [written[key]])
        tile[key] = rows
        op("t", reads, [key], fn)

    def mm(reads, bank, out, lhs, rhs, start=True, stop=True, rows=None):
        tensor(reads, bank, rows, lambda e: e.matmul(out, lhs, rhs, start, stop))

    def transpose(reads, bank, out, in_):
        tensor(reads + ["ident"], bank, None, lambda e: e.transpose(out, in_, T.ident[:, :]))

    def blocks_turned(reads, writes, out, in_):
        op("v", reads, writes, lambda e: e.transpose(out, in_))

    def iota(key, out, pattern, base, per_row=0):
        op("g", [], [key], lambda e: e.iota(out, pattern, base, per_row, allow_small_or_imprecise_dtypes=True))
        return key

    def fill(win, a, b, reads=("fb", "fc"), src=None, value=0.0):
        key = "%s@%d" % (win, a)
        op("s", list(reads), [key], lambda e: e.activation(T[win][:, a:b], src or T.fbc[:, a:b], IDENT, bias=value, scale=0.0))
        return key

    def send(arr, sent, dests, reads, src, land):
        before("g", reads, [])
        trs = []
        for i, r in enumerate(dests):
            rid, pid = topo.addr(cores[r], core)
            eng = topo.engines(core, cores[r])
            n = len(eng) // len(dests)
            trs.append(RemoteDMATransfer(
                dst_ids=[DstId(rid=rid, pnc=pid)], dma_engine_mask=sum(1 << e for e in eng[n * i:n * i + n]),
                remote_sem=T.sem[arr], srcs=[src(i, r)], dsts=[land], alu_op=0))
            for name in (arr, sent):
                count[name] = count.get(name, 0) + n
        g.remote_dma_fused(trs, local_sem=T.sem[sent])
        written[arr] = (arr, count[arr])
        written[sent] = (sent, count[sent])

    def in_turns(*chains):
        for k in range(max(len(c) for c in chains)):
            for c in chains:
                if k < len(c):
                    c[k]()

    def nothing():
        pass

    PS = [T["ps%d" % b] for b in range(8)]

    def next_table(n, src, reads):
        nx, key = T["nx%d" % n], "nx%d" % n
        for k in range(8):
            dma("y", "dn", reads, None, nx[16 * k:16 * k + 15, :], src(slice(16 * k + 1, 16 * k + 16), 0, 16))
        dma("y", "dn", [], None, nx[15::16, 0:15], src(slice(0, 128, 16), 1, 16))
        dma("y", "dn", ["neg"], key, nx[15::16, 15:16], T.neg[0:8, 0:1])

    dma("y", "dl", [], "li", T.li[:, 0:16], T.lb[:, :])
    dma("s", "dl", [], "li", T.li[:, 16:32], T.lc[:, :])
    for k in range(4):
        dma("y", "db", [], "fb", T.fbc[16 * k:16 * k + 16, :], T.fb[:, :])
        dma("s", "dc", [], "fc", T.fbc[64 + 16 * k:80 + 16 * k, :], T.fc[:, :])
    for k, x in enumerate((T.xa, T.xc, T.xb, T.ob)):
        dma("y", "dx", [], "xi", T.xi[:, 16 * k:16 * k + 16], x[:, :])
    dma("y", "dv", [], "v8", T.v8[:, :], T.v[:, :])
    dma("y", "dm", [], "lai", T.lai[:, :], T.la[:, :])

    op("g", [], ["pi"], lambda e: e.iota(T.pi[:, 0:1], [[0, 1]], 0, 1))
    iota("jm", T.jm[:, :], [[0, 8], [1, 16]], 0)
    iota("pf", T.pf[:, 0:1], [[0, 1]], 0, 1)
    op("g", [], ["neg"], lambda e: e.iota(T.neg[:, 0:1], [[0, 1]], -1, 0))
    iota("trb", T.trb[:, :], [[16, 16]], 2048)
    iota("l1a", T.land1[:, 0:16], [[0, 16]], 0)
    iota("l1b", T.land1[:, 1552:1568], [[0, 16]], 0)
    iota("idx", T.idx[:, :], [[1, 256]], 0)
    iota("j32", T.j32[:, :], [[0, 5], [1, 32]], 0)
    next_table(1, lambda rows, a, b: T.xa[rows, a:b], [])
    pf = T.pf[:, 0:1]
    W1 = [fill("win1", a, a + 128, ["jm"], T.jm[:, :]) for a in (0, 128)]
    for a in (256, 512):
        W1.append(fill("win1", a, a + 256, W1[0:2], T.win1[:, 0:256]))

    def bits(j, m):
        ts(["pi"], ["pm%d" % j], T.pm[:, j:j + 1], T.pi[:, 0:1], m, None, Op.bitwise_and)

    def col(j):
        return T.pq[:, j:j + 1]

    def more(j, factor, key, out, okey, last):
        ts(["pm%d" % j, key], [okey], out, T.pm[:, j:j + 1], factor, last, Op.mult, Op.add)

    bits(0, 31)
    bits(2, 2)
    bits(4, 48)
    copy("v", ["pm0"], ["p31"], col(0), T.pm[:, 0:1])
    bits(3, 12)
    bits(5, 64)
    ts(["jm", "p31"], ["su0"], T.su[:, 0:128], T.jm[:, :], col(0), None, Op.is_equal)
    ts(["jm", "p31"], ["su1"], T.su[:, 128:256], T.jm[:, :], 16.0, col(0), Op.add, Op.is_equal)
    more(2, 3.0, "pf", col(2), "o1", pf)
    ts(["pm4"], ["o2"], col(10), T.pm[:, 4:5], -0.875, None, Op.mult)

    def to_groups(reads, bank, out, r, table):
        rows = slice(32 * (r // 2), 32 * (r // 2) + 32)
        mm(reads + ["su%d" % (r % 2)], bank, out, T.su[rows, 128 * (r % 2):128 * (r % 2) + 128], table[rows, :], rows=rows)

    copy("v", ["li"], ["lh"], T.lh[:, :], T.li[:, :])
    more(3, 7.0, "o1", col(11), "o3", col(2))
    more(5, -0.75, "o2", col(14), "o4", col(10))
    side = n_ranks // 2
    turn1 = [r for r in turn if r // side != me // side] + [r for r in turn if r // side == me // side]
    for i, r in enumerate(turn1 + [me]):
        to_groups(["lh"], i // 2, PS[i // 2][:, 32 * (i % 2):32 * (i % 2) + 32], r, T.lh)
    bits(1, 15)
    ts(["o3", "o4"], ["ofu"], T.ofu[:, 0:1], col(11), col(14), None, Op.add)
    for k in range(4):
        copy("vs"[k % 2], ["P%d" % k], ["rep%d" % k], T.rep[:, 64 * k:64 * k + 64], PS[k][:, 0:64])
    for h in range(2):
        copy("v", ["rep%d" % (2 * h), "rep%d" % (2 * h + 1), "ofu"], ["lt%d" % h], T["lt"][:, 16 * h:16 * h + 16],
             T.rep[:, 128 * h:128 * h + 128].indirect(T.ofu[:, 0:1]))
    W1.append(fill("win1", 768, 1024, W1[0:2], T.win1[:, 0:256]))
    copy("v", ["pm1"], ["p15"], col(1), T.pm[:, 1:2])
    ts(["p31"], ["ph"], col(4), col(0), 16.0, None, Op.is_ge)

    own1 = T.land1[:, 528 + 64 * me:528 + 64 * me + 64]

    def columns(q, key, out, a, n):
        copy(q, ["fb", "fc", "lt%d" % (a // 16)], [key], out, T.fbc[:, :].indirect(T["lt"][:, a:a + n]))

    columns("v", "sb1a", T.sb1[:, 0:128], 0, 8)
    columns("s", "sb1b", T.sb1[:, 128:256], 8, 8)
    send("arr10", "sent1", turn1[0:4], ["sb1a", "sb1b"], lambda i, r: T.sb1[:, 64 * i:64 * i + 64], own1)
    columns("s", "sb1c", T.sb1[:, 256:448], 16, 12)
    send("arr11", "sent1", turn1[4:6], ["sb1c"], lambda i, r: T.sb1[:, 256 + 64 * i:320 + 64 * i], own1)
    send("arr12", "sent1", turn1[6:7], ["sb1c"], lambda i, r: T.sb1[:, 384:448], own1)
    columns("s", "own1", own1, 28, 4)
    for k in range(8):
        dma("y", "da", ["sent1"], "fa", T.far[16 * k:16 * k + 16, :], T.fa[:, :])
    for h in range(2):
        dma("y", "df", [], "fa2", T.fa2[:, 128 * h:128 * h + 128], T.fa[8 * h:8 * h + 8, :])
    iota("em", T.em[:, :], [[1, 8], [0, 16]], 0, -1)
    iota("iot", T.iot[:, :], [[1, 2048]], 0)

    def ends(x, key, n):
        eq, nu, of = "eq%d" % n, "nu%d" % n, "of%d" % n
        return [lambda: tt(["nx%d" % n, key], [eq], T[eq][:, :], T["nx%d" % n][:, :], x, Op.is_equal),
                lambda: copy("v", [eq], [nu], T[nu][:, :], T[eq][:, :]),
                lambda: tt(["tr", eq], ["td"], T.td[:, :], T.tr[:, :], T[eq][:, :], Op.mult),
                lambda: tt(["td", key], ["td"], T.td[:, :], T.td[:, :], x, Op.max),
                lambda: copy("v", ["td"], [of], T[of][:, :], T.td[:, :])]

    def same(q, n):
        at = 272 * (n - 1)
        copy(q, ["nu%d" % n, "idx"], ["same%d" % n], T.same[:, at + 1:at + 257], T.idx[:, 0:16].indirect(T["nu%d" % n][:, :]))

    x3 = T.xi[:, 0:48]
    e1 = ends(T.xi[:, 0:16], "xi", 1)
    ts(["xi"], ["xk"], T.xk[:, :], x3, 96, None, Op.bitwise_and)
    ts(["xi"], ["xq"], T.xq[:, :], x3, 1920, None, Op.bitwise_and)
    ts(["j32", "p31"], ["z32"], T.z32[:, :], T.j32[:, 0:144], col(0), None, Op.is_equal)
    ts(["xk"], ["x1"], T.e1[:, :], T.xk[:, :], 15.0, None, Op.mult)
    ts(["xq"], ["x2"], T.e2[:, :], T.xq[:, :], -0.75, None, Op.mult)
    ts(["pm4"], ["bl1"], col(3), T.pm[:, 4:5], -32.0, 528.0, Op.mult, Op.add)
    tt(["x1", "xi"], ["x1"], T.e1[:, :], T.e1[:, :], x3, Op.add)
    e1[0]()
    tt(["x1", "x2"], ["xh"], T.xh[:, :], T.e1[:, 16:48], T.e2[:, 16:48], Op.add)
    op("s", ["trb", "p15"], ["tr"], lambda e: e.activation(T.tr[:, :], T.trb[:, :], IDENT, bias=col(1)))
    wsel0 = fill("wsel", 0, 224)
    op("s", ["fb"], ["se"], lambda e: e.activation(T.same[:, 0::272], T.fbc[:, 0:2], COPY, scale=0.0))
    W1.append(fill("win1", 1024, 2048))
    for pair in range(4):
        rows = slice(32 * pair, 32 * pair + 32)
        for f in range(2):
            for a, b in PARTS1:
                at = 4 * a + (b - a) * pair
                mm(["xh", "z32"], 4 + f, PS[4 + f][:, at:at + b - a], T.z32[rows, 0:128],
                   T.xh[rows, 16 * (1 - f) + a:16 * (1 - f) + b], rows=rows)
    in_turns(e1[1:], [
        lambda: ts(["ph", "pf"], ["to"], col(8), col(4), 96.0, pf, Op.mult, Op.add),
        lambda: ts(["idx", "p31", wsel0], ["wsel"], T.wsel[:, 96:128], T.idx[:, 0:32], col(0), None, Op.is_equal),
        lambda: ts(["idx", "to"], ["swap"], T.swap[:, :], T.idx[:, :], -16.0, col(8), Op.add, Op.is_equal),
        lambda: ts(["em"], ["e8"], T.e8[:, :], T.em[:, :], 0.0, None, Op.is_equal)])
    mm(["e8", "v8"], 6, PS[6][:, 0:256], T.e8[:, :], T.v8[:, :], rows=slice(0, 8))
    for f in range(2):
        half = slice(64 * f, 64 * f + 64)
        op("s", ["P%d" % (4 + f), "bl1"], ["cu1%d" % f], lambda e: e.activation(
            T.cu1[half, :], PS[4 + f][half, 0:64], RELU, bias=T.pq[half, 3:4]))
    same("s", 1)
    tt(["x1", "x2"], ["xa"], T.e1[:, 0:16], T.e1[:, 0:16], T.e2[:, 0:16], Op.add)
    ts(["cu10", "cu11"], ["l1"], T.l1[:, :], T.cu1[:, :], 1552.0, None, Op.min)
    ts(["jm", "p15"], ["a16"], T.a16[:, :], T.jm[:, 0:16], col(1), None, Op.is_equal)
    copy("v", ["xa"], ["xu0"], T.xu[:, 0:16], T.e1[:, 0:16])
    copy("v", ["xi"], ["xu1"], T.xu[:, 16:48], T.xi[:, 32:64])
    ts(["idx", "ph"], ["c256"], T.pq[:, 6:8], T.idx[:, 0:2], col(4), 256.0, Op.is_equal, Op.mult)
    copy("s", ["P6"], ["vf"], T.vf[:, :], PS[6][:, 0:256])
    copy("v", ["lai"], ["lah"], T.lah[:, :], T.lai[:, :])
    for h in range(2):
        ts(["xi", "c256"], ["ob2%d" % h], T.ob2[:, h::2], T.xi[:, 48:64], col(6 + h), None, Op.add)

    L1 = ["l1a", "l1b", "l1"]
    for c, (keys, ranks) in enumerate(((["arr10"], turn1[0:4]), (["arr11"], turn1[4:6]), (["arr12", "own1"], [turn1[6], me]))):
        a, n = 64 * min(ranks), 64 * len(ranks)
        for u in range(2):
            bank = 2 * c + u
            mm(keys + ["swap"], bank, PS[bank][:, 0:n], T.swap[:, 128 * u:128 * u + 128], T.land1[:, 528 + a:528 + a + n])
            L1.append("side%d%d" % (c, u))
            copy("vs"[u], ["P%d" % bank], [L1[-1]], T.land1[:, 16 + 1024 * u + a:16 + 1024 * u + a + n], PS[bank][:, 0:n])

    def gather1(q, part, r0, r1):
        a, b = PARTS1[part]
        lo, n = 4 * a + (b - a) * r0, (b - a) * (r1 - r0)
        copy(q, L1, ["gb1%d%d" % (part, r) for r in range(r0, r1)], T.gb1[:, 16 * lo:16 * (lo + n)],
             T.land1[:, :].indirect(T.l1[:, lo:lo + n]))

    def select1(part):
        a, b = PARTS1[part]
        for r in range(4):
            lo = 16 * (4 * a + (b - a) * r)
            for f in (1, 0):
                rows = slice(64 * f, 64 * f + 64)
                mm(["gb1%d%d" % (part, r), "wsel"], 2 * part + f, PS[2 * part + f][:, 0:16 * (b - a)],
                   T.wsel[rows, 96 - 32 * r:224 - 32 * r], T.gb1[rows, lo:lo + 16 * (b - a)], r == 0, r == 3, rows)

    def run_sums(n, part, a, b):
        c, p, at = T["c%d" % n], T["p%d" % n], 272 * (n - 1)
        first = [] if a == 0 else ["c%d%d" % (n, part - 1)]
        op("v", ["p%d%d" % (n, part), "same%d" % n, "se"] + first, ["c%d%d" % (n, part)],
           lambda e: e.tensor_tensor_scan(c[:, a:b], T.same[:, at + a:at + b], p[:, a:b], c[:, a - 1:a] if a else 0.0,
                                          Op.mult, Op.add))

    def products1(part):
        a, b = (16 * x for x in PARTS1[part])
        return [lambda: tt(["P%d" % (2 * part + 1), "vf"], ["w%d" % part], T.w[:, a:b], PS[2 * part + 1][:, 0:b - a],
                           T.vf[:, a:b], Op.mult),
                lambda: tt(["P%d" % (2 * part), "w%d" % part], ["p1%d" % part], T.p1[:, a:b], PS[2 * part][:, 0:b - a],
                           T.w[:, a:b], Op.mult),
                lambda: run_sums(1, part, a, b)]

    for r in range(4):
        gather1("vs"[r % 2], 0, r, r + 1)
    select1(0)
    for q, r0, r1 in (("v", 0, 1), ("s", 1, 3), ("s", 3, 4)):
        gather1(q, 1, r0, r1)
    select1(1)
    p, q = products1(0), products1(1)
    for step in (p[0], p[1], q[0], p[2], q[1], q[2]):
        step()

    def add_groups(bank, out, data, keys):
        mm(keys + ["a16"], bank, out, data, T.a16[:, :])

    def exchange(x, data, keys, out, between):
        sb, land = T["sb%d" % x], T["land%d" % x]
        for c, dests in enumerate(CALLS + [[me]]):
            for i, r in enumerate(dests):
                for b in range(2):
                    add_groups(c, PS[c][:, 32 * i + b:32 * i + 32:2], data[:, 256 * r + 128 * b:256 * r + 128 * b + 128], keys(r, b))
            a, n = 32 * dests[0], 32 * len(dests)
            if c == len(CALLS):
                out(["P%d" % c], ["own%d" % x], land[:, a:a + n], PS[c][:, 0:n], a, n)
            else:
                out(["P%d" % c], ["sb%d%d" % (x, c)], sb[:, a:a + n], PS[c][:, 0:n], a, n)
                send("arr3%d" % c if x == 3 else "arr%d" % x, "sent", dests, ["sb%d%d" % (x, c)],
                     lambda i, r: sb[:, 32 * r:32 * r + 32], land[:, 32 * me:32 * me + 32])
            between[c]()

    def as_it_is(reads, writes, dst, src, a, n):
        copy("v", reads, writes, dst, src)

    def gathers(win, keys, table, order):
        def piece(q, r, a, b):
            copy(q, keys, ["gb%d%d" % (r, k) for k in range(a, b)], T.gb[:, 256 * r + 128 * a:256 * r + 128 * b],
                 win.indirect(table[:, 16 * r + 8 * a:16 * r + 8 * b]))
        for k in range(2):
            piece("v", order[k], 0, 1)
            piece("s", order[k], 1, 2)
        for k in range(2, 5):
            piece("vss"[k - 2], order[k], 0, 2)
        return lambda: [piece("vss"[k - 5], order[k], 0, 2) for k in range(5, 8)]

    ORDER = [r for dests in CALLS for r in dests] + [me]

    def gathered(r, b):
        return ["gb%d%d" % (r, b)]

    def turn_back(x):
        land, r = T["land%d" % x], T["r%d" % x]
        for b in range(2):
            transpose(["arr%d" % x, "own%d" % x], 5 + b, PS[5 + b][:, 0:128], land[:, b::2])
            copy("vs"[b], ["P%d" % (5 + b)], ["r%d%d" % (x, b)], r[:, 128 * b:128 * b + 128], PS[5 + b][:, 0:128])

    def inverse(n, lst, none, bank, turner):
        inv = T["inv%d" % n]
        return [lambda a=0, b=2: copy("v", [lst, "idx"] + none, ["inv%d" % n], inv[:, :].indirect(T[lst][:, 8 * a:8 * b]),
                                      T.idx[:, 128 * a:128 * b]),
                lambda: [mm(["inv%d" % n, "sel8"], bank, PS[bank][:, a:128:16], inv[:, a:2048:16], T.sel8[:, :]) for a in range(16)],
                lambda q: copy(q, ["P%d" % bank], ["invt"], T.invt[:, :], PS[bank][:, 0:128]),
                lambda: mm(["invt", turner], bank, PS[bank][:, 128:256], T.invt[:, :], T[turner][:, :]),
                lambda: copy("v", ["P%d" % bank], ["l%d" % n], T["l%d" % n][:, :], PS[bank][:, 128:256])]

    W2 = [fill("win2", 0, 512)]
    copy("s", ["iot", "xu0", "xu1"], ["xx"], T.xx[:, :], T.iot[:, :].indirect(T.xu[:, 0:32]))
    copy("s", ["xx", "ob20", "ob21"], ["ex"], T.ex[:, :], T.xx[:, :].indirect(T.ob2[:, :]))

    def lists_b():
        ts(["t2", "p15"], ["pick"], T.pick[:, 0:2], T.pq[:, 12:14], col(1), 32.0, Op.add, Op.mult)
        copy("v", ["P7"], ["lau"], T.lau[:, :], PS[7][:, 0:128])

    def lists_c():
        copy("v", ["li"], ["lbu"], T.lbu[:, :], T.li[:, 0:16])
        ts(["idx", "pf"], ["sel8"], T.sel8[:, :], T.idx[:, 0:128:16], pf, None, Op.is_equal)

    def lists_d():
        ts(["j32", "p31"], ["a32"], T.a32[:, :], T.j32[:, 0:32], col(0), None, Op.is_equal)
        ts(["idx", "pf"], ["identb"], T.identb[:, :], T.idx[:, 0:128], pf, None, Op.is_equal)

    def lists_e():
        ts(["p31", "pf"], ["b16"], col(9), col(0), pf, 16.0, Op.subtract, Op.mult)

    for r in range(8):
        to_groups(["lah"], 7, PS[7][:, 16 * r:16 * r + 16], r, T.lah)
    copy("v", ["c10", "c11", "of1"] + W1, ["win1"], T.win1[:, :].indirect(T.of1[:, :]), T.c1[:, :])
    copy("v", ["lai"], ["lau0"], T.lau0[:, :], T.lai[:, :])
    ts(["idx", "ph"], ["t2"], T.pq[:, 12:14], T.idx[:, 0:2], col(4), 0.5, Op.is_equal, Op.mult)
    ts(["idx", "pf"], ["ident"], T.ident[:, :], T.idx[:, 0:128], pf, None, Op.is_equal)
    copy("s", ["fa", "lau0"], ["fag"], T.fag[:, :], T.far[:, :].indirect(T.lau0[:, :]))
    W2.append(fill("win2", 512, 2048))
    copy("s", ["w0", "w1", "xu1"], ["w2"], T.w2[:, :], T.w[:, :].indirect(T.xu[:, 32:48]))
    exchange(2, T.win1, lambda r, b: ["win1"], as_it_is,
             (lists_b, lists_c, lists_d, lists_e, lambda: blocks_turned(["ex"], ["xt"], T.xt[:, :], T.ex[:, :])))
    iota("dpb", T.dpb[:, :], [[32, 2], [1, 2], [0, 2]], 0)
    iota("r3a", T.r3[:, 0:8], [[0, 8]], 0)
    iota("r3b", T.r3[:, 520:528], [[0, 8]], 0)
    iota("c2z", T.c2[:, 256:264], [[0, 8]], 0)
    none2 = [iota("inv2@0", T.inv2[:, 0:768], [[0, 768]], 256)]
    for b in range(2):
        transpose(["fag"], 0, PS[0][:, 128 * b:128 * b + 128], T.fag[:, 128 * b:128 * b + 128])
    ts(["b16"], ["bl3"], col(15), col(9), 8.0, None, Op.add)
    copy("v", ["xt", "pick"], ["xf2"], T.xf2[:, :], T.xt[:, :].indirect(T.pick[:, 0:2]))
    next_table(2, lambda rows, a, b: T.xf2[rows, 16 + a:16 + b], ["xf2"])
    e2 = ends(T.xf2[:, 16:32], "xf2", 2)
    for b in range(2):
        copy("sv"[b], ["P0"], ["fat%d" % b], T.fat[:, b::2], PS[0][:, 128 * b:128 * b + 128])
    ts(["dpb", "p15"], ["dpo"], T.dpo[:, :], T.dpb[:, :], col(1), col(1), Op.add, Op.add)
    none2.append(fill("inv2", 768, 1664, value=256.0))
    copy("v", ["xf2"], ["xah"], T.xah[:, :], T.xf2[:, 0:16])
    blocks_turned(["w2"], ["w2t"], T.w2t[:, :], T.w2[:, :])

    turn_back(2)
    for b in range(2):
        copy("v", ["r2%d" % b, "lau0"] + W2, ["win2"],
             T.win2[:, :].indirect(T.lau0[:, 8 * b:8 * b + 8]), T.r2[:, 128 * b:128 * b + 128])
    none2.append(fill("inv2", 1664, 2048, value=256.0))
    for P in range(4):
        rows = slice(32 * P, 32 * P + 32)
        for h in range(2):
            mm(["xah", "z32"], 7, PS[7][:, 2 * P + h:64:8], T.z32[rows, 16:144], T.xah[rows, h::2], rows=rows)
    rest = gathers(T.win2[:, :], ["win2", "lau"], T.lau, ORDER)
    ends2 = inverse(2, "of2", none2, 5, "identb")

    exchange(3, T.gb, gathered,
             lambda reads, writes, dst, src, a, m: tt(reads + ["fat0", "fat1"], writes, dst, src, T.fat[:, a:a + m], Op.mult),
             (lambda: (rest(), op("s", ["P7", "bl3"], ["cu3"],
                                  lambda e: e.activation(T.cu3[:, :], PS[7][:, 0:64], RELU, bias=col(15)))),
              lambda: (e2[0](), e2[2]()),
              lambda: (e2[1](), e2[3](), same("s", 2)),
              e2[4],
              lambda: (ends2[0](), ts(["cu3"], ["l3"], T.l3[:, :], T.cu3[:, :], 520.0, None, Op.min))))
    iota("r4z", T.r4[:, 256:264], [[0, 8]], 0)
    iota("pb0", T.pb[:, :], [[2, 16], [32, 4], [1, 2]], 0)
    none4 = [iota("inv4@0", T.inv4[:, :], [[0, 2048]], 256)]

    def rows_a(blocks):
        for blk in blocks:
            add_groups(7, PS[7][:, blk:256:16], T.win2[:, 128 * blk:128 * blk + 128], ["win2"])

    rows_a(range(8))
    ends2[1]()

    R3 = ["r3a", "r3b", "l3"]
    for key, dests in [("arr30", CALLS[0]), ("arr31", CALLS[1]), ("own3", [me]), ("arr32", CALLS[2]), ("arr33", CALLS[3])]:
        a, n = dests[0], len(dests)
        copy("s", [key, "dpo"], ["dup" + key], T.dup3[:, 64 * a:64 * (a + n)],
             T.land3[:, 32 * a:32 * (a + n)].indirect(T.dpo[:, 0:4 * n]))
        blocks_turned(["dup" + key], ["r3" + key], T.r3[:, 8 + 64 * a:8 + 64 * (a + n)], T.dup3[:, 64 * a:64 * (a + n)])
        R3.append("r3" + key)
    ends2[2]("s")
    ends2[3]()

    def gather3(q, a, b):
        copy(q, R3, ["gb3%d" % C for C in range(a, b)], T.gb3[:, 128 * a:128 * b], T.r3[:, :].indirect(T.l3[:, 8 * a:8 * b]))

    for q, a, b in (("v", 0, 1), ("s", 1, 2), ("v", 2, 3), ("s", 3, 4), ("v", 4, 6), ("s", 6, 8)):
        gather3(q, a, b)
    for part, (a, b) in enumerate(PARTS3):
        for C in range(a, b):
            mm(["gb3%d" % C, "a32"], part, PS[part][:, 32 * (C - a):32 * (C - a) + 32], T.gb3[:, 128 * C:128 * C + 128], T.a32[:, :])
    rows_a(range(8, 16))

    def products2(part):
        a, b = (32 * x for x in PARTS3[part])
        return [lambda: tt(["P%d" % part, "w2t"], ["pt%d" % part], T.pt[:, a:b], PS[part][:, 0:b - a], T.w2t[:, a:b], Op.mult),
                lambda: blocks_turned(["pt%d" % part], ["p2%d" % part], T.p2[:, a:b], T.pt[:, a:b]),
                lambda: run_sums(2, part, a, b)]

    p, q = products2(0), products2(1)
    for step in (p[0], ends2[4], p[1], q[0], p[2], q[1], q[2]):
        step()

    slots = inverse(4, "lbu", none4, 0, "pb")
    rest = gathers(T.c2[:, :], ["c20", "c21", "c2z", "l2"], T.l2, ORDER)
    exchange(4, T.gb, gathered, as_it_is, (
        lambda: (rest(), copy("s", ["P7"], ["ta"], T.ta[:, :], PS[7][:, 0:256])),
        lambda: slots[0](0, 1), nothing, lambda: slots[0](1, 2),
        lambda: ts(["pb0", "pf"], ["pb"], T.pb[:, :], T.pb[:, :], pf, None, Op.is_equal)))
    slots[1]()
    slots[2]("s")

    slots[3]()
    slots[4]()
    turn_back(4)
    for h in range(2):
        transpose(["ta"], 7, PS[7][:, 128 * h:128 * h + 128], T.ta[:, 128 * h:128 * h + 128])
    for q, a, b in [("vs"[k % 2], k, k + 1) for k in range(4)] + [("vs"[k % 2], 2 * k, 2 * k + 2) for k in range(2, 8)]:
        copy(q, ["r40", "r41", "r4z", "l4"], ["gb%d%d" % divmod(m, 2) for m in range(a, b)], T.gb[:, 128 * a:128 * b],
             T.r4[:, :].indirect(T.l4[:, 8 * a:8 * b]))
    tt(["P7", "fa2"], ["yas"], T.yas[:, :], PS[7][:, 0:256], T.fa2[:, :], Op.mult)
    for h in range(2):
        dma("y", "do", ["yas"], None, T.ya[8 * h:8 * h + 8, :], T.yas[:, 128 * h:128 * h + 128])
    for m in range(16):
        u, C = divmod(m, 8)
        bank = 2 + C // 6
        add_groups(bank, PS[bank][:, 32 * C + u:32 * C + 32:2], T.gb[:, 128 * m:128 * m + 128], gathered(*divmod(m, 2)))
    for k, (a, b) in enumerate(((0, 192), (192, 256))):
        blocks_turned(["P%d" % (2 + k)], ["ybs%d" % k], T.ybs[:, a:b], PS[2 + k][:, a:b])
    for P in range(4):
        dma("ys"[P % 2], "do", ["ybs0", "ybs1"], None, T.yb[:, 512 * P:512 * P + 512], T.ybs[32 * P:32 * P + 32, :])
    for name in sorted(count):
        g.wait_ge(T.sem[name], count[name])
